import numpy as np
import ml_dtypes


def mxq(x, axis, fmt="e4m3"):
    dtype, down = {"e4m3": (ml_dtypes.float8_e4m3fn, 7), "e5m2": (ml_dtypes.float8_e5m2, 14)}[fmt]
    v = np.moveaxis(np.asarray(x, np.float32).astype(ml_dtypes.bfloat16).astype(np.float64), axis, -1)
    blocks = v.reshape(v.shape[:-1] + (-1, 32))
    amax = np.abs(blocks).max(-1, keepdims=True)
    byte = np.maximum(np.where(amax > 0, np.frexp(amax)[1] - 1 + 127, 0) - down, 1)
    scale = np.exp2(byte - 127.0)
    codes = (blocks / scale).astype(np.float32).astype(dtype).astype(np.float64)
    return np.moveaxis((codes * scale).reshape(v.shape), -1, axis)


WIDE = False


def mx_kscale(k):
    if not WIDE:
        return np.ones(k)
    levels = np.array([10, -10, 5, -5, 0])
    if k % 512:
        return np.exp2(np.random.permutation(np.resize(levels, k // 32))).repeat(32)
    a = np.empty((k // 512, 16))
    for p in range(k // 512):
        a[p, :8] = np.random.permutation(np.resize(levels, 8))
        for g in range(8):
            far = levels[np.abs(levels - a[p, g]) >= 10]
            a[p, g + 8] = far[np.random.randint(len(far))]
    return np.exp2(a.ravel()).repeat(32)


def f64(x):
    return np.asarray(x).astype(np.float64)


def striped(idx):
    return np.tile(idx.reshape(-1, 16).T, (8, 1)).astype(np.uint16)


def unstriped(offs):
    return offs[:16].T.reshape(-1).astype(np.int64)


def pack_weight(w):
    k, n = w.shape
    w = f64(np.asarray(w, np.float32).astype(ml_dtypes.bfloat16)).reshape(k // 32, 32, n)
    amax = np.abs(w).max(1)
    byte = np.clip(np.where(amax > 0, np.frexp(amax)[1] - 1 + 127 - 7, 1), 1, 254)
    scaled = (w * np.exp2(127.0 - byte)[:, None, :]).reshape(k, n).astype(np.float32)
    words = np.ascontiguousarray(scaled.reshape(k // 512, 128, 4, n).transpose(0, 1, 3, 2)).astype(ml_dtypes.float8_e4m3fn).view(np.uint8)
    return words, np.ascontiguousarray(byte.astype(np.uint8).reshape(k // 512, 16, n))


def unpack_weight(words, scales):
    g, p, n, _ = words.shape
    vals = np.ascontiguousarray(words).view(ml_dtypes.float8_e4m3fn).astype(np.float64) * np.repeat(np.exp2(scales.astype(np.float64) - 127.0), 8, axis=1)[..., None]
    return vals.transpose(0, 1, 3, 2).reshape(g * 512, n)


def planes(y):
    n, m = y.shape
    v = y.astype(np.float32).astype(ml_dtypes.bfloat16).astype(np.float64).reshape(n // 32, 32, m)
    top = np.abs(v).max(1)
    byte = np.clip(np.where(top > 0, np.frexp(top)[1] - 1 + 127 - 7, 1), 1, 254)
    codes = (v * np.exp2(127.0 - byte)[:, None, :]).reshape(n, m).astype(np.float32).astype(ml_dtypes.float8_e4m3fn).view(np.uint8)
    words = codes.reshape(n // 512, 128, 4, m).transpose(0, 1, 3, 2)
    return np.ascontiguousarray(words), np.ascontiguousarray(byte.astype(np.uint8).reshape(n // 512, 16, m))


K, T, S, D, V, H, N = 512, 2048, 1024, 4, 512, 512, 512
P = 2 ** 7


def setup_inputs():
    n = np.random.standard_normal
    s = mx_kscale(K)[:, None]
    u = mx_kscale(H)
    near = np.random.permutation(S)
    packed_xT = pack_weight(n((K, T)) * s)
    return {
        "x_words": packed_xT[0],
        "x_scales": packed_xT[1],
        "w1": (n((K, H)) / np.sqrt(K) / s * u).astype(np.float32),
        "w2": (n((H, N)) / np.sqrt(H) / u[:, None]).astype(np.float32),
        "gate": (np.tile(np.random.uniform(0.1, 0.6, (D, 1, V)), (1, P, 1))).astype(np.float32),
        "ref": (n((H, V)) * u[:, None]).astype(np.float32),
        "offs": striped(np.random.permutation(T)[:S]),
        "pos1": striped(near[:V]),
        "pos2": striped(near[V:]),
        "pos3": striped(np.random.permutation(S)[:V]),
        "pos4": striped(np.random.permutation(S)[:V]),
    }


def reference(x_words, x_scales, w1, w2, gate, ref, offs, pos1, pos2, pos3, pos4):
    xq = unpack_weight(x_words, x_scales)[:, unstriped(offs)]
    f = mxq(f64(w1), 0, "e4m3").T @ xq
    e = f64(ref) - (f[:, unstriped(pos1)] * f64(gate)[0, :1] + f[:, unstriped(pos2)] * f64(gate)[1, :1] + f[:, unstriped(pos3)] * f64(gate)[2, :1] + f[:, unstriped(pos4)] * f64(gate)[3, :1])
    out_0 = mxq(f64(w2), 0, "e4m3").T @ mxq(e, 0, "e4m3")
    return (out_0,) + planes(out_0)

@@ -1,0 +1,206 @@
+from contextlib import ExitStack
+
+import concourse.mybir as mybir
+from concourse.masks import make_identity
+
+K, T, S, D, V, H, N = 512, 2048, 1024, 4, 512, 512, 512
+FLOPS = 2 * K * H * S + 2 * H * N * V
+
+F32 = mybir.dt.float32
+BF16 = mybir.dt.bfloat16
+I32 = mybir.dt.int32
+U32 = mybir.dt.uint32
+U16 = mybir.dt.uint16
+U8 = mybir.dt.uint8
+FP8X4 = mybir.dt.float8_e4m3fn_x4
+COPY = mybir.ActivationFunctionType.Copy
+MULT = mybir.AluOpType.mult
+
+P = 128
+PACK = 4
+STRIPE = 16
+TILES = H // P
+WORD_PIECES = ((0, 512), (512, 768), (768, 1024))
+HALVES = ((0, 512), (512, 1024))
+W1_PIECES = ((0, 1), (1, 2), (2, 4))
+PARTS = ((0, 384), (384, 512))
+
+
+def tile_picked_zwarp_none_po_kernel(
+    tc, x_words, x_scales, w1, w2, gate, ref, offs, pos1, pos2, pos3, pos4, out_0, out_1, out_2
+):
+    nc = tc.nc
+    with ExitStack() as ctx:
+        held = ctx.enter_context(tc.tile_pool(name="held", bufs=1))
+        ring = ctx.enter_context(tc.tile_pool(name="ring", bufs=6))
+        work = ctx.enter_context(tc.tile_pool(name="work", bufs=2))
+        acc_banks = ctx.enter_context(tc.psum_pool(name="acc_banks", bufs=3))
+        sum_banks = ctx.enter_context(tc.psum_pool(name="sum_banks", bufs=3))
+        back_banks = ctx.enter_context(tc.psum_pool(name="back_banks", bufs=2))
+
+        scale_table = held.tile([P, T], U8, align_bytes=64)
+        nc.gpsimd.memset(scale_table[:].bitcast(I32), 0)
+        picks = held.tile([P, S // STRIPE], U16)
+        nc.sync.dma_start(picks[:], offs)
+        w1_rows = w1.rearrange("(p j) h -> p j h", j=PACK)
+        w1_first = held.tile([P, PACK, P], F32)
+        nc.sync.dma_start(out=w1_first[:], in_=w1_rows[:, :, 0:P])
+        corners = [held.tile([P, V // STRIPE], U16, name="corner%d" % d) for d in range(D)]
+        nc.sync.dma_start(corners[0][:], pos1)
+        for q in range(4):
+            nc.sync.dma_start(
+                out=scale_table[32 * q : 32 * q + 4, :].bitcast(I32),
+                in_=x_scales[0, 4 * q : 4 * q + 4, :].bitcast(I32),
+            )
+        word_table = held.tile([P, T], I32, align_bytes=64)
+        nc.sync.dma_start(out=word_table[:], in_=x_words[0].rearrange("p c r -> p (c r)").bitcast(I32))
+        w1_rest = held.tile([P, PACK, H - P], F32)
+        nc.sync.dma_start(out=w1_rest[:], in_=w1_rows[:, :, P:H])
+
+        gates = []
+        for d, pos in enumerate((pos1, pos2, pos3, pos4)):
+            if d > 0:
+                nc.sync.dma_start(corners[d][:], pos)
+            weight = held.tile([P, V], F32, name="gate%d" % d)
+            nc.sync.dma_start(out=weight[:], in_=gate[d])
+            gates.append(weight)
+        ref_rows = ref.rearrange("(t p) v -> p t v", p=P)
+        ref_first = held.tile([P, 1, V], F32)
+        nc.sync.dma_start(out=ref_first[:], in_=ref_rows[:, 0:1, :])
+        ref_rest = held.tile([P, TILES - 1, V], F32)
+        nc.sync.dma_start(out=ref_rest[:], in_=ref_rows[:, 1:TILES, :])
+        w2_raw = held.tile([P, PACK, N], F32)
+        nc.sync.dma_start(out=w2_raw[:], in_=w2.rearrange("(p j) n -> p j n", j=PACK))
+
+        identity = held.tile([P, P], F32)
+        make_identity(nc, identity[:])
+
+        x_bytes = held.tile([P, S], U8, align_bytes=64)
+        nc.vector.tensor_copy(x_bytes[:], scale_table[:].indirect(picks[:]))
+        x_codes = held.tile([P, S], U32, align_bytes=64)
+        for a, b in WORD_PIECES:
+            nc.vector.tensor_copy(
+                x_codes[:, a:b], word_table[:].bitcast(U32).indirect(picks[:, a // STRIPE : b // STRIPE])
+            )
+
+        features = []
+        for t0, t1 in W1_PIECES:
+            width = (t1 - t0) * P
+            source = w1_first[:] if t0 == 0 else w1_rest[:, :, (t0 - 1) * P : (t1 - 1) * P]
+            grouped = held.tile([P, width * PACK], BF16, name="w1_grouped%d" % t0, align_bytes=64)
+            nc.scalar.activation(
+                grouped[:].rearrange("p (c i j) -> p c j i", i=4, j=PACK),
+                source.rearrange("p j (c i) -> p c j i", i=4),
+                COPY,
+            )
+            codes = held.tile([P, width], U32, name="w1_codes%d" % t0, align_bytes=64)
+            scales = held.tile([P, width], U8, name="w1_scales%d" % t0, align_bytes=64)
+            nc.vector.quantize_mx(out=codes[:].bitcast(FP8X4), scales=scales[:], in_=grouped[:])
+            for t in range(t0, t1):
+                cols = slice((t - t0) * P, (t - t0 + 1) * P)
+                feature = held.tile([P, S], F32, name="feature%d" % t)
+                for a, b in WORD_PIECES if t == 0 else HALVES:
+                    acc = acc_banks.tile([P, b - a], F32, name="acc")
+                    nc.tensor.matmul_mx(
+                        out=acc[:],
+                        lhsT=codes[:, cols].bitcast(FP8X4),
+                        lhsT_scale=scales[:, cols],
+                        rhs=x_codes[:, a:b].bitcast(FP8X4),
+                        rhs_scale=x_bytes[:, a:b],
+                        start=True,
+                        stop=True,
+                    )
+                    nc.scalar.activation(feature[:, a:b], acc[:], COPY, scale=-1.0)
+                features.append(feature)
+
+        w2_grouped = held.tile([P, N * PACK], BF16, align_bytes=64)
+        nc.scalar.copy(
+            w2_grouped[:].rearrange("p (t m j) -> p m j t", t=PACK, j=PACK),
+            w2_raw[:].rearrange("p j (m t) -> p m j t", t=PACK),
+        )
+        w2_codes = held.tile([P, N], U32, align_bytes=64)
+        w2_scales = held.tile([P, N], U8, align_bytes=64)
+        nc.vector.quantize_mx(out=w2_codes[:].bitcast(FP8X4), scales=w2_scales[:], in_=w2_grouped[:])
+
+        out_rows = out_0.rearrange("(p t) v -> p t v", t=PACK)
+        out_words = out_1[0].rearrange("p c r -> p (c r)").bitcast(I32)
+        y_scales = held.tile([P, V], U8, align_bytes=64)
+
+        for v0, v1 in PARTS:
+            width = v1 - v0
+            chunks = width // P
+            last = v1 == V
+            e_pairs = held.tile([P, chunks * H], BF16, name="e_pairs%d" % v0, align_bytes=64)
+            for t in range(TILES):
+                ref_tile = ref_first[:, 0, :] if t == 0 else ref_rest[:, t - 1, :]
+                total = sum_banks.tile([P, chunks, P], F32, name="total")
+                for c in range(chunks):
+                    nc.tensor.matmul(
+                        total[:, c, :], ref_tile[:, v0 + c * P : v0 + (c + 1) * P], identity[:],
+                        is_transpose=True, start=(c == 0), stop=False,
+                    )
+                for d in range(D):
+                    term = ring.tile([P, width], F32, name="term")
+                    nc.vector.tensor_tensor(
+                        term[:],
+                        features[t][:].indirect(corners[d][:, v0 // STRIPE : v1 // STRIPE]),
+                        gates[d][:, v0:v1],
+                        MULT,
+                    )
+                    for c in range(chunks):
+                        nc.tensor.matmul(
+                            total[:, c, :], term[:, c * P : (c + 1) * P], identity[:],
+                            is_transpose=True, start=False, stop=(d == D - 1 and c == chunks - 1),
+                        )
+                nc.scalar.copy(
+                    e_pairs[:].rearrange("v (c u p e) -> v c u p e", u=2, p=P, e=2)[:, :, :, 32 * t : 32 * (t + 1), :],
+                    total[:].rearrange("v c (p u e) -> v c u p e", u=2, e=2),
+                )
+
+            y = held.tile([P, PACK, width], F32, name="y%d" % v0)
+            y_codes = held.tile([P, width], I32, name="y_codes%d" % v0, align_bytes=64)
+            e_words = e_pairs[:].bitcast(F32)
+            for c in range(chunks):
+                cols = slice(c * P, (c + 1) * P)
+                back = back_banks.tile([P, 2, P], F32, name="back")
+                for u in range(2):
+                    nc.tensor.transpose(back[:, u, :], e_words[:, (2 * c + u) * P : (2 * c + u + 1) * P], identity[:])
+                e_grouped = work.tile([P, P * PACK], BF16, name="e_grouped", align_bytes=64)
+                nc.scalar.copy(
+                    e_grouped[:].bitcast(F32).rearrange("p (v u) -> p v u", u=2),
+                    back[:].rearrange("p u v -> p v u"),
+                )
+                e_codes = work.tile([P, P], U32, name="e_codes", align_bytes=64)
+                e_scales = work.tile([P, P], U8, name="e_scales", align_bytes=64)
+                nc.vector.quantize_mx(out=e_codes[:].bitcast(FP8X4), scales=e_scales[:], in_=e_grouped[:])
+                acc = acc_banks.tile([P, PACK, P], F32, name="acc")
+                for t in range(PACK):
+                    nc.tensor.matmul_mx(
+                        out=acc[:, t, :],
+                        lhsT=w2_codes[:, t * P : (t + 1) * P].bitcast(FP8X4),
+                        lhsT_scale=w2_scales[:, t * P : (t + 1) * P],
+                        rhs=e_codes[:].bitcast(FP8X4),
+                        rhs_scale=e_scales[:],
+                        start=True,
+                        stop=True,
+                    )
+                y_grouped = work.tile([P, P * PACK], BF16, name="y_grouped", align_bytes=64)
+                y_view = y_grouped[:].rearrange("p (v t) -> p v t", t=PACK)
+                if last:
+                    nc.vector.tensor_copy(y_view, acc[:].rearrange("p t v -> p v t"))
+                else:
+                    nc.scalar.copy(y_view, acc[:].rearrange("p t v -> p v t"))
+                nc.scalar.copy(y[:, :, cols], acc[:])
+                nc.vector.quantize_mx(
+                    out=y_codes[:, cols].bitcast(FP8X4),
+                    scales=y_scales[:, v0 + c * P : v0 + (c + 1) * P],
+                    in_=y_grouped[:],
+                )
+            (nc.scalar if last else nc.sync).dma_start(out=out_rows[:, :, v0:v1], in_=y[:])
+            nc.sync.dma_start(out=out_words[:, v0:v1], in_=y_codes[:])
+
+        for q in range(4):
+            (nc.sync if q < 2 else nc.scalar).dma_start(
+                out=out_2[0, 4 * q : 4 * q + 4, :].bitcast(I32),
+                in_=y_scales[32 * q : 32 * q + 4, :].bitcast(I32),
+            )

@@ -23,7 +23,15 @@ TILES = H // P
 WORD_PIECES = ((0, 512), (512, 768), (768, 1024))
 HALVES = ((0, 512), (512, 1024))
 W1_PIECES = ((0, 1), (1, 2), (2, 4))
-PARTS = ((0, 384), (384, 512))
+GROUPS = ((0, 256), (256, 384), (384, 512))
+HELD_BACK = {(1, 384, 2): (0, 7), (3, 384, 1): (1, 3)}
+STEPS = (
+    (0, 0, 512), (1, 0, 384),
+    (2, 0, 256), (3, 0, 256),
+    (2, 256, 384), (3, 256, 384),
+    (1, 384, 512), (2, 384, 512), (3, 384, 512),
+)
+GATHERS = [(t, v0, d) for t, v0, v1 in STEPS for d in range(D)]
 
 
 def tile_picked_zwarp_none_po_kernel(
@@ -33,20 +41,16 @@ def tile_picked_zwarp_none_po_kernel(
     with ExitStack() as ctx:
         held = ctx.enter_context(tc.tile_pool(name="held", bufs=1))
         ring = ctx.enter_context(tc.tile_pool(name="ring", bufs=6))
-        work = ctx.enter_context(tc.tile_pool(name="work", bufs=2))
         acc_banks = ctx.enter_context(tc.psum_pool(name="acc_banks", bufs=3))
-        sum_banks = ctx.enter_context(tc.psum_pool(name="sum_banks", bufs=3))
-        back_banks = ctx.enter_context(tc.psum_pool(name="back_banks", bufs=2))
+        turn_banks = ctx.enter_context(tc.psum_pool(name="turn_banks", bufs=1))
 
         scale_table = held.tile([P, T], U8, align_bytes=64)
         nc.gpsimd.memset(scale_table[:].bitcast(I32), 0)
         picks = held.tile([P, S // STRIPE], U16)
         nc.sync.dma_start(picks[:], offs)
-        w1_rows = w1.rearrange("(p j) h -> p j h", j=PACK)
-        w1_first = held.tile([P, PACK, P], F32)
-        nc.sync.dma_start(out=w1_first[:], in_=w1_rows[:, :, 0:P])
         corners = [held.tile([P, V // STRIPE], U16, name="corner%d" % d) for d in range(D)]
         nc.sync.dma_start(corners[0][:], pos1)
+        nc.sync.dma_start(corners[1][:], pos2)
         for q in range(4):
             nc.sync.dma_start(
                 out=scale_table[32 * q : 32 * q + 4, :].bitcast(I32),
@@ -54,19 +58,21 @@ def tile_picked_zwarp_none_po_kernel(
             )
         word_table = held.tile([P, T], I32, align_bytes=64)
         nc.sync.dma_start(out=word_table[:], in_=x_words[0].rearrange("p c r -> p (c r)").bitcast(I32))
-        w1_rest = held.tile([P, PACK, H - P], F32)
-        nc.sync.dma_start(out=w1_rest[:], in_=w1_rows[:, :, P:H])
-
-        gates = []
-        for d, pos in enumerate((pos1, pos2, pos3, pos4)):
-            if d > 0:
-                nc.sync.dma_start(corners[d][:], pos)
-            weight = held.tile([P, V], F32, name="gate%d" % d)
-            nc.sync.dma_start(out=weight[:], in_=gate[d])
-            gates.append(weight)
+        w1_rows = w1.rearrange("(p j) h -> p j h", j=PACK)
+        w1_first = held.tile([P, PACK, P], F32, tag="w1_first", align_bytes=64)
+        nc.sync.dma_start(out=w1_first[:], in_=w1_rows[:, :, 0:P])
+        gates = [held.tile([P, V], F32, name="gate%d" % d) for d in range(D)]
+        nc.sync.dma_start(out=gates[0][:], in_=gate[0])
         ref_rows = ref.rearrange("(t p) v -> p t v", p=P)
         ref_first = held.tile([P, 1, V], F32)
         nc.sync.dma_start(out=ref_first[:], in_=ref_rows[:, 0:1, :])
+        nc.sync.dma_start(out=gates[1][:], in_=gate[1])
+        w1_rest = held.tile([P, PACK, H - P], F32)
+        nc.sync.dma_start(out=w1_rest[:], in_=w1_rows[:, :, P:H])
+        nc.sync.dma_start(corners[2][:], pos3)
+        nc.sync.dma_start(corners[3][:], pos4)
+        nc.sync.dma_start(out=gates[2][:], in_=gate[2])
+        nc.sync.dma_start(out=gates[3][:], in_=gate[3])
         ref_rest = held.tile([P, TILES - 1, V], F32)
         nc.sync.dma_start(out=ref_rest[:], in_=ref_rows[:, 1:TILES, :])
         w2_raw = held.tile([P, PACK, N], F32)
@@ -77,25 +83,44 @@ def tile_picked_zwarp_none_po_kernel(
 
         x_bytes = held.tile([P, S], U8, align_bytes=64)
         nc.vector.tensor_copy(x_bytes[:], scale_table[:].indirect(picks[:]))
-        x_codes = held.tile([P, S], U32, align_bytes=64)
-        for a, b in WORD_PIECES:
-            nc.vector.tensor_copy(
-                x_codes[:, a:b], word_table[:].bitcast(U32).indirect(picks[:, a // STRIPE : b // STRIPE])
-            )
+        x_codes = []
+
+        def gather_words(half, tag):
+            picked = held.tile([P, S // 2], U32, name="x_codes%d" % half, tag=tag, align_bytes=64)
+            for a, b in WORD_PIECES:
+                if a // (S // 2) == half:
+                    nc.vector.tensor_copy(
+                        picked[:, a % (S // 2) : a % (S // 2) + b - a],
+                        word_table[:].bitcast(U32).indirect(picks[:, a // STRIPE : b // STRIPE]),
+                    )
+            x_codes.append(picked)
+
+        gather_words(0, "x_codes0")
 
         features = []
         for t0, t1 in W1_PIECES:
             width = (t1 - t0) * P
             source = w1_first[:] if t0 == 0 else w1_rest[:, :, (t0 - 1) * P : (t1 - 1) * P]
-            grouped = held.tile([P, width * PACK], BF16, name="w1_grouped%d" % t0, align_bytes=64)
+            grouped = held.tile(
+                [P, width * PACK], BF16, name="w1_grouped%d" % t0,
+                tag="w1_shared%d" % t0, align_bytes=64,
+            )
             nc.scalar.activation(
                 grouped[:].rearrange("p (c i j) -> p c j i", i=4, j=PACK),
                 source.rearrange("p j (c i) -> p c j i", i=4),
                 COPY,
             )
-            codes = held.tile([P, width], U32, name="w1_codes%d" % t0, align_bytes=64)
-            scales = held.tile([P, width], U8, name="w1_scales%d" % t0, align_bytes=64)
+            codes = held.tile(
+                [P, width], U32, name="w1_codes%d" % t0,
+                tag="w1_shared1" if t0 == 0 else "w1_codes%d" % t0, align_bytes=64,
+            )
+            scales = held.tile(
+                [P, width], U8, name="w1_scales%d" % t0,
+                tag="w1_shared2" if t0 == 0 else "w1_scales%d" % t0, align_bytes=64,
+            )
             nc.vector.quantize_mx(out=codes[:].bitcast(FP8X4), scales=scales[:], in_=grouped[:])
+            if t0 == 0:
+                gather_words(1, "w1_first")
             for t in range(t0, t1):
                 cols = slice((t - t0) * P, (t - t0 + 1) * P)
                 feature = held.tile([P, S], F32, name="feature%d" % t)
@@ -105,13 +130,17 @@ def tile_picked_zwarp_none_po_kernel(
                         out=acc[:],
                         lhsT=codes[:, cols].bitcast(FP8X4),
                         lhsT_scale=scales[:, cols],
-                        rhs=x_codes[:, a:b].bitcast(FP8X4),
+                        rhs=x_codes[a // (S // 2)][:, a % (S // 2) : a % (S // 2) + b - a].bitcast(FP8X4),
                         rhs_scale=x_bytes[:, a:b],
                         start=True,
                         stop=True,
                     )
-                    nc.scalar.activation(feature[:, a:b], acc[:], COPY, scale=-1.0)
+                    if t == 0 and (a, b) == WORD_PIECES[1]:
+                        nc.vector.tensor_scalar_mul(feature[:, a:b], acc[:], -1.0)
+                    else:
+                        nc.scalar.activation(feature[:, a:b], acc[:], COPY, scale=-1.0)
                 features.append(feature)
+
 
         w2_grouped = held.tile([P, N * PACK], BF16, align_bytes=64)
         nc.scalar.copy(
@@ -126,78 +155,141 @@ def tile_picked_zwarp_none_po_kernel(
         out_words = out_1[0].rearrange("p c r -> p (c r)").bitcast(I32)
         y_scales = held.tile([P, V], U8, align_bytes=64)
 
-        for v0, v1 in PARTS:
+        e_pairs = [
+            held.tile([P, (v1 - v0) // P * H], BF16, name="e_pairs%d" % v0, align_bytes=64) for v0, v1 in GROUPS
+        ]
+
+        late_slots = {}
+        bank_uses = []
+
+        def next_bank(shape):
+            bank_uses.append(shape)
+            return turn_banks.tile(shape, F32, name="turn", tag="turn%d" % (len(bank_uses) % 3))
+
+        def difference(t, v0, v1):
             width = v1 - v0
             chunks = width // P
-            last = v1 == V
-            e_pairs = held.tile([P, chunks * H], BF16, name="e_pairs%d" % v0, align_bytes=64)
-            for t in range(TILES):
-                ref_tile = ref_first[:, 0, :] if t == 0 else ref_rest[:, t - 1, :]
-                total = sum_banks.tile([P, chunks, P], F32, name="total")
+            ref_tile = ref_first[:, 0, :] if t == 0 else ref_rest[:, t - 1, :]
+            total = next_bank([P, chunks, P]) if t > 1 or v0 > 0 else turn_banks.tile([P, chunks, P], F32, name="early%d" % t)
+            for d in range(D):
+                if (t, v0, d) in HELD_BACK:
+                    g, count = HELD_BACK[(t, v0, d)]
+                    late = held.tile([P, count * P], F32, name="late_terms", tag="e_grouped%d" % g, align_bytes=64)
+                    first = GATHERS.index((t, v0, d))
+                    for n in range(count):
+                        late_slots[GATHERS[first + n]] = late[:, n * P : (n + 1) * P]
+                term = late_slots[(t, v0, d)] if (t, v0, d) in late_slots else ring.tile([P, width], F32, name="term")[:]
+                nc.vector.tensor_tensor(
+                    term,
+                    features[t][:].indirect(corners[d][:, v0 // STRIPE : v1 // STRIPE]),
+                    gates[d][:, v0:v1],
+                    MULT,
+                )
                 for c in range(chunks):
                     nc.tensor.matmul(
-                        total[:, c, :], ref_tile[:, v0 + c * P : v0 + (c + 1) * P], identity[:],
-                        is_transpose=True, start=(c == 0), stop=False,
+                        total[:, c, :], term[:, c * P : (c + 1) * P], identity[:],
+                        is_transpose=True, start=(d == 0 and c == 0), stop=(d == D - 1 and c == chunks - 1),
                     )
-                for d in range(D):
-                    term = ring.tile([P, width], F32, name="term")
-                    nc.vector.tensor_tensor(
-                        term[:],
-                        features[t][:].indirect(corners[d][:, v0 // STRIPE : v1 // STRIPE]),
-                        gates[d][:, v0:v1],
-                        MULT,
-                    )
+                if d == 0:
                     for c in range(chunks):
                         nc.tensor.matmul(
-                            total[:, c, :], term[:, c * P : (c + 1) * P], identity[:],
-                            is_transpose=True, start=False, stop=(d == D - 1 and c == chunks - 1),
+                            total[:, c, :], ref_tile[:, v0 + c * P : v0 + (c + 1) * P], identity[:],
+                            is_transpose=True, start=False, stop=False,
                         )
-                nc.scalar.copy(
-                    e_pairs[:].rearrange("v (c u p e) -> v c u p e", u=2, p=P, e=2)[:, :, :, 32 * t : 32 * (t + 1), :],
-                    total[:].rearrange("v c (p u e) -> v c u p e", u=2, e=2),
-                )
-
-            y = held.tile([P, PACK, width], F32, name="y%d" % v0)
-            y_codes = held.tile([P, width], I32, name="y_codes%d" % v0, align_bytes=64)
-            e_words = e_pairs[:].bitcast(F32)
-            for c in range(chunks):
-                cols = slice(c * P, (c + 1) * P)
-                back = back_banks.tile([P, 2, P], F32, name="back")
-                for u in range(2):
-                    nc.tensor.transpose(back[:, u, :], e_words[:, (2 * c + u) * P : (2 * c + u + 1) * P], identity[:])
-                e_grouped = work.tile([P, P * PACK], BF16, name="e_grouped", align_bytes=64)
-                nc.scalar.copy(
-                    e_grouped[:].bitcast(F32).rearrange("p (v u) -> p v u", u=2),
-                    back[:].rearrange("p u v -> p v u"),
-                )
-                e_codes = work.tile([P, P], U32, name="e_codes", align_bytes=64)
-                e_scales = work.tile([P, P], U8, name="e_scales", align_bytes=64)
-                nc.vector.quantize_mx(out=e_codes[:].bitcast(FP8X4), scales=e_scales[:], in_=e_grouped[:])
-                acc = acc_banks.tile([P, PACK, P], F32, name="acc")
-                for t in range(PACK):
-                    nc.tensor.matmul_mx(
-                        out=acc[:, t, :],
-                        lhsT=w2_codes[:, t * P : (t + 1) * P].bitcast(FP8X4),
-                        lhsT_scale=w2_scales[:, t * P : (t + 1) * P],
-                        rhs=e_codes[:].bitcast(FP8X4),
-                        rhs_scale=e_scales[:],
-                        start=True,
-                        stop=True,
+            for g, (g0, g1) in enumerate(GROUPS):
+                if v0 <= g0 and g1 <= v1:
+                    pairs = e_pairs[g][:].rearrange("v (c u p e) -> v c u p e", u=2, p=P, e=2)
+                    nc.scalar.copy(
+                        pairs[:, :, :, 32 * t : 32 * (t + 1), :],
+                        total[:, (g0 - v0) // P : (g1 - v0) // P, :].rearrange("v c (p u e) -> v c u p e", u=2, e=2),
                     )
-                y_grouped = work.tile([P, P * PACK], BF16, name="y_grouped", align_bytes=64)
-                y_view = y_grouped[:].rearrange("p (v t) -> p v t", t=PACK)
-                if last:
-                    nc.vector.tensor_copy(y_view, acc[:].rearrange("p t v -> p v t"))
-                else:
-                    nc.scalar.copy(y_view, acc[:].rearrange("p t v -> p v t"))
-                nc.scalar.copy(y[:, :, cols], acc[:])
-                nc.vector.quantize_mx(
-                    out=y_codes[:, cols].bitcast(FP8X4),
-                    scales=y_scales[:, v0 + c * P : v0 + (c + 1) * P],
-                    in_=y_grouped[:],
+
+        e_planes = {}
+        results = {}
+
+        def turn_back(g):
+            v0, v1 = GROUPS[g]
+            width = v1 - v0
+            chunks = width // P
+            e_words = e_pairs[g][:].bitcast(F32)
+            back = next_bank([P, chunks, 2, P])
+            for c in range(chunks):
+                for u in range(2):
+                    nc.tensor.transpose(back[:, c, u, :], e_words[:, (2 * c + u) * P : (2 * c + u + 1) * P], identity[:])
+            e_grouped = held.tile([P, width * PACK], BF16, name="e_grouped", tag="e_grouped%d" % g, align_bytes=64)
+            nc.scalar.copy(
+                e_grouped[:].bitcast(F32).rearrange("p (c v u) -> p c v u", v=P, u=2),
+                back[:].rearrange("p c u v -> p c v u"),
+            )
+            e_codes = held.tile([P, width], U32, name="e_codes%d" % g, align_bytes=64)
+            e_scales = held.tile([P, width], U8, name="e_scales%d" % g, align_bytes=64)
+            nc.vector.quantize_mx(out=e_codes[:].bitcast(FP8X4), scales=e_scales[:], in_=e_grouped[:])
+            e_planes[g] = (e_codes, e_scales)
+            results[g] = held.tile([P, PACK, width], F32, name="y%d" % v0)
+
+        def second_product(g, c):
+            v0, v1 = GROUPS[g]
+            last = v1 == V
+            e_codes, e_scales = e_planes[g]
+            y = results[g]
+            cols = slice(c * P, (c + 1) * P)
+            acc = next_bank([P, PACK, P])
+            for t in range(PACK):
+                nc.tensor.matmul_mx(
+                    out=acc[:, t, :],
+                    lhsT=w2_codes[:, t * P : (t + 1) * P].bitcast(FP8X4),
+                    lhsT_scale=w2_scales[:, t * P : (t + 1) * P],
+                    rhs=e_codes[:, cols].bitcast(FP8X4),
+                    rhs_scale=e_scales[:, cols],
+                    start=True,
+                    stop=True,
                 )
-            (nc.scalar if last else nc.sync).dma_start(out=out_rows[:, :, v0:v1], in_=y[:])
-            nc.sync.dma_start(out=out_words[:, v0:v1], in_=y_codes[:])
+            if last:
+                y_grouped = held.tile([P, P * PACK], BF16, name="last_grouped", align_bytes=64)
+                nc.vector.tensor_copy(
+                    y_grouped[:].rearrange("p (v t) -> p v t", t=PACK), acc[:].rearrange("p t v -> p v t")
+                )
+            nc.scalar.copy(y[:, :, cols], acc[:])
+            if v0 + (c + 1) * P == v1:
+                (nc.scalar if last else nc.sync).dma_start(out=out_rows[:, :, v0:v1], in_=y[:])
+            if last:
+                y_codes = held.tile([P, P], I32, name="last_codes", align_bytes=64)
+                nc.vector.quantize_mx(out=y_codes[:].bitcast(FP8X4), scales=y_scales[:, v0:v1], in_=y_grouped[:])
+                nc.sync.dma_start(out=out_words[:, v0:v1], in_=y_codes[:])
+
+        def early_planes():
+            width = GROUPS[-1][0]
+            y_grouped = held.tile([P, width * PACK], BF16, name="early_grouped", tag="e_grouped1", align_bytes=64)
+            y_codes = held.tile([P, width], I32, name="early_codes", align_bytes=64)
+            for g, (v0, v1) in enumerate(GROUPS[:-1]):
+                y = results[g]
+                nc.vector.tensor_copy(
+                    y_grouped[:, v0 * PACK : v1 * PACK].rearrange("p (c i t) -> p c t i", i=4, t=PACK),
+                    y[:].rearrange("p t (c i) -> p c t i", i=4),
+                )
+            for v0, v1 in GROUPS[:-1]:
+                nc.vector.quantize_mx(
+                    out=y_codes[:, v0:v1].bitcast(FP8X4), scales=y_scales[:, v0:v1], in_=y_grouped[:, v0 * PACK : v1 * PACK]
+                )
+            nc.sync.dma_start(out=out_words[:, 0:width], in_=y_codes[:])
+
+        difference(0, 0, 512)
+        difference(1, 0, 384)
+        difference(2, 0, 256)
+        difference(3, 0, 256)
+        difference(2, 256, 384)
+        turn_back(0)
+        difference(3, 256, 384)
+        difference(1, 384, 512)
+        turn_back(1)
+        second_product(0, 0)
+        difference(2, 384, 512)
+        second_product(0, 1)
+        difference(3, 384, 512)
+        second_product(1, 0)
+        early_planes()
+        turn_back(2)
+        second_product(2, 0)
 
         for q in range(4):
             (nc.sync if q < 2 else nc.scalar).dma_start(

@@ -24,7 +24,7 @@ WORD_PIECES = ((0, 512), (512, 768), (768, 1024))
 HALVES = ((0, 512), (512, 1024))
 W1_PIECES = ((0, 1), (1, 2), (2, 4))
 GROUPS = ((0, 256), (256, 384), (384, 512))
-HELD_BACK = {(1, 384, 2): (0, 7), (3, 384, 1): (1, 3)}
+HELD_BACK = {(2, 384, 0): (0, 8)}
 STEPS = (
     (0, 0, 512), (1, 0, 384),
     (2, 0, 256), (3, 0, 256),
@@ -40,7 +40,7 @@ def tile_picked_zwarp_none_po_kernel(
     nc = tc.nc
     with ExitStack() as ctx:
         held = ctx.enter_context(tc.tile_pool(name="held", bufs=1))
-        ring = ctx.enter_context(tc.tile_pool(name="ring", bufs=6))
+        ring = ctx.enter_context(tc.tile_pool(name="ring", bufs=8))
         acc_banks = ctx.enter_context(tc.psum_pool(name="acc_banks", bufs=3))
         turn_banks = ctx.enter_context(tc.psum_pool(name="turn_banks", bufs=1))
 
@@ -61,7 +61,7 @@ def tile_picked_zwarp_none_po_kernel(
         w1_rows = w1.rearrange("(p j) h -> p j h", j=PACK)
         w1_first = held.tile([P, PACK, P], F32, tag="w1_first", align_bytes=64)
         nc.sync.dma_start(out=w1_first[:], in_=w1_rows[:, :, 0:P])
-        gates = [held.tile([P, V], F32, name="gate%d" % d) for d in range(D)]
+        gates = [held.tile([P, V], F32, name="gate%d" % d, tag="gate%d" % d, align_bytes=64) for d in range(D)]
         nc.sync.dma_start(out=gates[0][:], in_=gate[0])
         ref_rows = ref.rearrange("(t p) v -> p t v", p=P)
         ref_first = held.tile([P, 1, V], F32)
@@ -221,7 +221,9 @@ def tile_picked_zwarp_none_po_kernel(
                 e_grouped[:].bitcast(F32).rearrange("p (c v u) -> p c v u", v=P, u=2),
                 back[:].rearrange("p c u v -> p c v u"),
             )
-            e_codes = held.tile([P, width], U32, name="e_codes%d" % g, align_bytes=64)
+            e_codes = held.tile(
+                [P, width], U32, name="e_codes%d" % g, tag="gate%d" % (D - 1) if g == 1 else "e_codes%d" % g, align_bytes=64
+            )
             e_scales = held.tile([P, width], U8, name="e_scales%d" % g, align_bytes=64)
             nc.vector.quantize_mx(out=e_codes[:].bitcast(FP8X4), scales=e_scales[:], in_=e_grouped[:])
             e_planes[g] = (e_codes, e_scales)
@@ -233,45 +235,34 @@ def tile_picked_zwarp_none_po_kernel(
             e_codes, e_scales = e_planes[g]
             y = results[g]
             cols = slice(c * P, (c + 1) * P)
-            acc = next_bank([P, PACK, P])
-            for t in range(PACK):
-                nc.tensor.matmul_mx(
-                    out=acc[:, t, :],
-                    lhsT=w2_codes[:, t * P : (t + 1) * P].bitcast(FP8X4),
-                    lhsT_scale=w2_scales[:, t * P : (t + 1) * P],
-                    rhs=e_codes[:, cols].bitcast(FP8X4),
-                    rhs_scale=e_scales[:, cols],
-                    start=True,
-                    stop=True,
-                )
-            if last:
-                y_grouped = held.tile([P, P * PACK], BF16, name="last_grouped", align_bytes=64)
-                nc.vector.tensor_copy(
-                    y_grouped[:].rearrange("p (v t) -> p v t", t=PACK), acc[:].rearrange("p t v -> p v t")
-                )
-            nc.scalar.copy(y[:, :, cols], acc[:])
+            per_bank = PACK // 2 if last else PACK
+            for t0 in range(0, PACK, per_bank):
+                acc = next_bank([P, per_bank, P])
+                for t in range(t0, t0 + per_bank):
+                    nc.tensor.matmul_mx(
+                        out=acc[:, t - t0, :],
+                        lhsT=w2_codes[:, t * P : (t + 1) * P].bitcast(FP8X4),
+                        lhsT_scale=w2_scales[:, t * P : (t + 1) * P],
+                        rhs=e_codes[:, cols].bitcast(FP8X4),
+                        rhs_scale=e_scales[:, cols],
+                        start=True,
+                        stop=True,
+                    )
+                nc.scalar.copy(y[:, t0 : t0 + per_bank, cols], acc[:])
             if v0 + (c + 1) * P == v1:
                 (nc.scalar if last else nc.sync).dma_start(out=out_rows[:, :, v0:v1], in_=y[:])
-            if last:
-                y_codes = held.tile([P, P], I32, name="last_codes", align_bytes=64)
-                nc.vector.quantize_mx(out=y_codes[:].bitcast(FP8X4), scales=y_scales[:, v0:v1], in_=y_grouped[:])
-                nc.sync.dma_start(out=out_words[:, v0:v1], in_=y_codes[:])
 
-        def early_planes():
-            width = GROUPS[-1][0]
-            y_grouped = held.tile([P, width * PACK], BF16, name="early_grouped", tag="e_grouped1", align_bytes=64)
-            y_codes = held.tile([P, width], I32, name="early_codes", align_bytes=64)
-            for g, (v0, v1) in enumerate(GROUPS[:-1]):
-                y = results[g]
-                nc.vector.tensor_copy(
-                    y_grouped[:, v0 * PACK : v1 * PACK].rearrange("p (c i t) -> p c t i", i=4, t=PACK),
-                    y[:].rearrange("p t (c i) -> p c t i", i=4),
-                )
-            for v0, v1 in GROUPS[:-1]:
-                nc.vector.quantize_mx(
-                    out=y_codes[:, v0:v1].bitcast(FP8X4), scales=y_scales[:, v0:v1], in_=y_grouped[:, v0 * PACK : v1 * PACK]
-                )
-            nc.sync.dma_start(out=out_words[:, 0:width], in_=y_codes[:])
+        def early_planes(g):
+            v0, v1 = GROUPS[g]
+            width = v1 - v0
+            y_grouped = held.tile([P, width * PACK], BF16, name="early_grouped", tag="e_grouped%d" % g, align_bytes=64)
+            y_codes = held.tile([P, width], I32, name="early_codes%d" % g, align_bytes=64)
+            nc.vector.tensor_copy(
+                y_grouped[:].rearrange("p (c i t) -> p c t i", i=4, t=PACK),
+                results[g][:].rearrange("p t (c i) -> p c t i", i=4),
+            )
+            nc.vector.quantize_mx(out=y_codes[:].bitcast(FP8X4), scales=y_scales[:, v0:v1], in_=y_grouped[:])
+            nc.sync.dma_start(out=out_words[:, v0:v1], in_=y_codes[:])
 
         difference(0, 0, 512)
         difference(1, 0, 384)
@@ -287,9 +278,11 @@ def tile_picked_zwarp_none_po_kernel(
         second_product(0, 1)
         difference(3, 384, 512)
         second_product(1, 0)
-        early_planes()
+        early_planes(0)
         turn_back(2)
+        early_planes(1)
         second_product(2, 0)
+        early_planes(2)
 
         for q in range(4):
             (nc.sync if q < 2 else nc.scalar).dma_start(

@@ -24,12 +24,12 @@ WORD_PIECES = ((0, 512), (512, 768), (768, 1024))
 HALVES = ((0, 512), (512, 1024))
 W1_PIECES = ((0, 1), (1, 2), (2, 4))
 GROUPS = ((0, 256), (256, 384), (384, 512))
-HELD_BACK = {(2, 384, 0): (0, 8)}
+HELD_BACK = {(1, 384, 2): (0, 6)}
 STEPS = (
     (0, 0, 512), (1, 0, 384),
     (2, 0, 256), (3, 0, 256),
-    (2, 256, 384), (3, 256, 384),
-    (1, 384, 512), (2, 384, 512), (3, 384, 512),
+    (2, 256, 512), (3, 256, 384),
+    (1, 384, 512), (3, 384, 512),
 )
 GATHERS = [(t, v0, d) for t, v0, v1 in STEPS for d in range(D)]
 
@@ -48,9 +48,11 @@ def tile_picked_zwarp_none_po_kernel(
         nc.gpsimd.memset(scale_table[:].bitcast(I32), 0)
         picks = held.tile([P, S // STRIPE], U16)
         nc.sync.dma_start(picks[:], offs)
+        w1_rows = w1.rearrange("(p j) h -> p j h", j=PACK)
+        w1_first = held.tile([P, PACK, P], F32)
+        nc.sync.dma_start(out=w1_first[:], in_=w1_rows[:, :, 0:P])
         corners = [held.tile([P, V // STRIPE], U16, name="corner%d" % d) for d in range(D)]
         nc.sync.dma_start(corners[0][:], pos1)
-        nc.sync.dma_start(corners[1][:], pos2)
         for q in range(4):
             nc.sync.dma_start(
                 out=scale_table[32 * q : 32 * q + 4, :].bitcast(I32),
@@ -58,21 +60,16 @@ def tile_picked_zwarp_none_po_kernel(
             )
         word_table = held.tile([P, T], I32, align_bytes=64)
         nc.sync.dma_start(out=word_table[:], in_=x_words[0].rearrange("p c r -> p (c r)").bitcast(I32))
-        w1_rows = w1.rearrange("(p j) h -> p j h", j=PACK)
-        w1_first = held.tile([P, PACK, P], F32, tag="w1_first", align_bytes=64)
-        nc.sync.dma_start(out=w1_first[:], in_=w1_rows[:, :, 0:P])
         gates = [held.tile([P, V], F32, name="gate%d" % d, tag="gate%d" % d, align_bytes=64) for d in range(D)]
         nc.sync.dma_start(out=gates[0][:], in_=gate[0])
         ref_rows = ref.rearrange("(t p) v -> p t v", p=P)
         ref_first = held.tile([P, 1, V], F32)
         nc.sync.dma_start(out=ref_first[:], in_=ref_rows[:, 0:1, :])
-        nc.sync.dma_start(out=gates[1][:], in_=gate[1])
         w1_rest = held.tile([P, PACK, H - P], F32)
         nc.sync.dma_start(out=w1_rest[:], in_=w1_rows[:, :, P:H])
-        nc.sync.dma_start(corners[2][:], pos3)
-        nc.sync.dma_start(corners[3][:], pos4)
-        nc.sync.dma_start(out=gates[2][:], in_=gate[2])
-        nc.sync.dma_start(out=gates[3][:], in_=gate[3])
+        for d, pos in ((1, pos2), (2, pos3), (3, pos4)):
+            nc.sync.dma_start(corners[d][:], pos)
+            nc.sync.dma_start(out=gates[d][:], in_=gate[d])
         ref_rest = held.tile([P, TILES - 1, V], F32)
         nc.sync.dma_start(out=ref_rest[:], in_=ref_rows[:, 1:TILES, :])
         w2_raw = held.tile([P, PACK, N], F32)
@@ -83,19 +80,11 @@ def tile_picked_zwarp_none_po_kernel(
 
         x_bytes = held.tile([P, S], U8, align_bytes=64)
         nc.vector.tensor_copy(x_bytes[:], scale_table[:].indirect(picks[:]))
-        x_codes = []
-
-        def gather_words(half, tag):
-            picked = held.tile([P, S // 2], U32, name="x_codes%d" % half, tag=tag, align_bytes=64)
-            for a, b in WORD_PIECES:
-                if a // (S // 2) == half:
-                    nc.vector.tensor_copy(
-                        picked[:, a % (S // 2) : a % (S // 2) + b - a],
-                        word_table[:].bitcast(U32).indirect(picks[:, a // STRIPE : b // STRIPE]),
-                    )
-            x_codes.append(picked)
-
-        gather_words(0, "x_codes0")
+        x_codes = held.tile([P, S], U32, align_bytes=64)
+        for a, b in WORD_PIECES:
+            nc.vector.tensor_copy(
+                x_codes[:, a:b], word_table[:].bitcast(U32).indirect(picks[:, a // STRIPE : b // STRIPE])
+            )
 
         features = []
         for t0, t1 in W1_PIECES:
@@ -119,18 +108,19 @@ def tile_picked_zwarp_none_po_kernel(
                 tag="w1_shared2" if t0 == 0 else "w1_scales%d" % t0, align_bytes=64,
             )
             nc.vector.quantize_mx(out=codes[:].bitcast(FP8X4), scales=scales[:], in_=grouped[:])
-            if t0 == 0:
-                gather_words(1, "w1_first")
             for t in range(t0, t1):
                 cols = slice((t - t0) * P, (t - t0 + 1) * P)
                 feature = held.tile([P, S], F32, name="feature%d" % t)
                 for a, b in WORD_PIECES if t == 0 else HALVES:
-                    acc = acc_banks.tile([P, b - a], F32, name="acc")
+                    if t == 0 and b == S:
+                        acc = turn_banks.tile([P, b - a], F32, name="first_acc", tag="early0")
+                    else:
+                        acc = acc_banks.tile([P, b - a], F32, name="acc")
                     nc.tensor.matmul_mx(
                         out=acc[:],
                         lhsT=codes[:, cols].bitcast(FP8X4),
                         lhsT_scale=scales[:, cols],
-                        rhs=x_codes[a // (S // 2)][:, a % (S // 2) : a % (S // 2) + b - a].bitcast(FP8X4),
+                        rhs=x_codes[:, a:b].bitcast(FP8X4),
                         rhs_scale=x_bytes[:, a:b],
                         start=True,
                         stop=True,
@@ -170,7 +160,12 @@ def tile_picked_zwarp_none_po_kernel(
             width = v1 - v0
             chunks = width // P
             ref_tile = ref_first[:, 0, :] if t == 0 else ref_rest[:, t - 1, :]
-            total = next_bank([P, chunks, P]) if t > 1 or v0 > 0 else turn_banks.tile([P, chunks, P], F32, name="early%d" % t)
+            total = next_bank([P, chunks, P]) if t > 1 or v0 > 0 else turn_banks.tile([P, chunks, P], F32, name="early", tag="early%d" % t)
+            for c in range(chunks):
+                nc.tensor.matmul(
+                    total[:, c, :], ref_tile[:, v0 + c * P : v0 + (c + 1) * P], identity[:],
+                    is_transpose=True, start=(c == 0), stop=False,
+                )
             for d in range(D):
                 if (t, v0, d) in HELD_BACK:
                     g, count = HELD_BACK[(t, v0, d)]
@@ -188,14 +183,8 @@ def tile_picked_zwarp_none_po_kernel(
                 for c in range(chunks):
                     nc.tensor.matmul(
                         total[:, c, :], term[:, c * P : (c + 1) * P], identity[:],
-                        is_transpose=True, start=(d == 0 and c == 0), stop=(d == D - 1 and c == chunks - 1),
+                        is_transpose=True, start=False, stop=(d == D - 1 and c == chunks - 1),
                     )
-                if d == 0:
-                    for c in range(chunks):
-                        nc.tensor.matmul(
-                            total[:, c, :], ref_tile[:, v0 + c * P : v0 + (c + 1) * P], identity[:],
-                            is_transpose=True, start=False, stop=False,
-                        )
             for g, (g0, g1) in enumerate(GROUPS):
                 if v0 <= g0 and g1 <= v1:
                     pairs = e_pairs[g][:].rearrange("v (c u p e) -> v c u p e", u=2, p=P, e=2)
@@ -237,7 +226,7 @@ def tile_picked_zwarp_none_po_kernel(
             cols = slice(c * P, (c + 1) * P)
             per_bank = PACK // 2 if last else PACK
             for t0 in range(0, PACK, per_bank):
-                acc = next_bank([P, per_bank, P])
+                acc = acc_banks.tile([P, per_bank, P], F32, name="acc") if g == 0 else next_bank([P, per_bank, P])
                 for t in range(t0, t0 + per_bank):
                     nc.tensor.matmul_mx(
                         out=acc[:, t - t0, :],
@@ -268,13 +257,12 @@ def tile_picked_zwarp_none_po_kernel(
         difference(1, 0, 384)
         difference(2, 0, 256)
         difference(3, 0, 256)
-        difference(2, 256, 384)
+        difference(2, 256, 512)
         turn_back(0)
         difference(3, 256, 384)
         difference(1, 384, 512)
         turn_back(1)
         second_product(0, 0)
-        difference(2, 384, 512)
         second_product(0, 1)
         difference(3, 384, 512)
         second_product(1, 0)

@@ -45,21 +45,21 @@ def tile_picked_zwarp_none_po_kernel(
         turn_banks = ctx.enter_context(tc.psum_pool(name="turn_banks", bufs=1))
 
         scale_table = held.tile([P, T], U8, align_bytes=64)
-        nc.gpsimd.memset(scale_table[:].bitcast(I32), 0)
+        nc.vector.memset(scale_table[:].bitcast(I32), 0)
         picks = held.tile([P, S // STRIPE], U16)
         nc.sync.dma_start(picks[:], offs)
         w1_rows = w1.rearrange("(p j) h -> p j h", j=PACK)
         w1_first = held.tile([P, PACK, P], F32)
-        nc.sync.dma_start(out=w1_first[:], in_=w1_rows[:, :, 0:P])
         corners = [held.tile([P, V // STRIPE], U16, name="corner%d" % d) for d in range(D)]
         nc.sync.dma_start(corners[0][:], pos1)
-        for q in range(4):
+        for r in range(4):
             nc.sync.dma_start(
-                out=scale_table[32 * q : 32 * q + 4, :].bitcast(I32),
-                in_=x_scales[0, 4 * q : 4 * q + 4, :].bitcast(I32),
+                out=scale_table[r:P:32, :].bitcast(I32),
+                in_=x_scales[0, r:16:4, :].bitcast(I32),
             )
         word_table = held.tile([P, T], I32, align_bytes=64)
         nc.sync.dma_start(out=word_table[:], in_=x_words[0].rearrange("p c r -> p (c r)").bitcast(I32))
+        nc.sync.dma_start(out=w1_first[:], in_=w1_rows[:, :, 0:P])
         gates = [held.tile([P, V], F32, name="gate%d" % d, tag="gate%d" % d, align_bytes=64) for d in range(D)]
         nc.sync.dma_start(out=gates[0][:], in_=gate[0])
         ref_rows = ref.rearrange("(t p) v -> p t v", p=P)
@@ -80,11 +80,16 @@ def tile_picked_zwarp_none_po_kernel(
 
         x_bytes = held.tile([P, S], U8, align_bytes=64)
         nc.vector.tensor_copy(x_bytes[:], scale_table[:].indirect(picks[:]))
-        x_codes = held.tile([P, S], U32, align_bytes=64)
-        for a, b in WORD_PIECES:
+        x_codes = {}
+
+        def gather_words(a, b, tag):
+            x_codes[a] = held.tile([P, b - a], U32, name="x_codes%d" % a, tag=tag, align_bytes=64)
             nc.vector.tensor_copy(
-                x_codes[:, a:b], word_table[:].bitcast(U32).indirect(picks[:, a // STRIPE : b // STRIPE])
+                x_codes[a][:], word_table[:].bitcast(U32).indirect(picks[:, a // STRIPE : b // STRIPE])
             )
+
+        for a, b in WORD_PIECES[:-1]:
+            gather_words(a, b, "x_codes%d" % a)
 
         features = []
         for t0, t1 in W1_PIECES:
@@ -108,6 +113,8 @@ def tile_picked_zwarp_none_po_kernel(
                 tag="w1_shared2" if t0 == 0 else "w1_scales%d" % t0, align_bytes=64,
             )
             nc.vector.quantize_mx(out=codes[:].bitcast(FP8X4), scales=scales[:], in_=grouped[:])
+            if t0 == 0:
+                gather_words(*WORD_PIECES[-1], "w1_shared0")
             for t in range(t0, t1):
                 cols = slice((t - t0) * P, (t - t0 + 1) * P)
                 feature = held.tile([P, S], F32, name="feature%d" % t)
@@ -116,15 +123,17 @@ def tile_picked_zwarp_none_po_kernel(
                         acc = turn_banks.tile([P, b - a], F32, name="first_acc", tag="early0")
                     else:
                         acc = acc_banks.tile([P, b - a], F32, name="acc")
-                    nc.tensor.matmul_mx(
-                        out=acc[:],
-                        lhsT=codes[:, cols].bitcast(FP8X4),
-                        lhsT_scale=scales[:, cols],
-                        rhs=x_codes[:, a:b].bitcast(FP8X4),
-                        rhs_scale=x_bytes[:, a:b],
-                        start=True,
-                        stop=True,
-                    )
+                    for pa, pb in WORD_PIECES:
+                        if a <= pa and pb <= b:
+                            nc.tensor.matmul_mx(
+                                out=acc[:, pa - a : pb - a],
+                                lhsT=codes[:, cols].bitcast(FP8X4),
+                                lhsT_scale=scales[:, cols],
+                                rhs=x_codes[pa][:].bitcast(FP8X4),
+                                rhs_scale=x_bytes[:, pa:pb],
+                                start=True,
+                                stop=True,
+                            )
                     if t == 0 and (a, b) == WORD_PIECES[1]:
                         nc.vector.tensor_scalar_mul(feature[:, a:b], acc[:], -1.0)
                     else:

@@ -15,23 +15,14 @@ U8 = mybir.dt.uint8
 FP8X4 = mybir.dt.float8_e4m3fn_x4
 COPY = mybir.ActivationFunctionType.Copy
 MULT = mybir.AluOpType.mult
+ADD = mybir.AluOpType.add
 
 P = 128
 PACK = 4
 STRIPE = 16
-TILES = H // P
+EARLY = 256
 WORD_PIECES = ((0, 512), (512, 768), (768, 1024))
 HALVES = ((0, 512), (512, 1024))
-W1_PIECES = ((0, 1), (1, 2), (2, 4))
-GROUPS = ((0, 256), (256, 384), (384, 512))
-HELD_BACK = {(1, 384, 2): (0, 6)}
-STEPS = (
-    (0, 0, 512), (1, 0, 384),
-    (2, 0, 256), (3, 0, 256),
-    (2, 256, 512), (3, 256, 384),
-    (1, 384, 512), (3, 384, 512),
-)
-GATHERS = [(t, v0, d) for t, v0, v1 in STEPS for d in range(D)]
 
 
 def tile_picked_zwarp_none_po_kernel(
@@ -41,15 +32,16 @@ def tile_picked_zwarp_none_po_kernel(
     with ExitStack() as ctx:
         held = ctx.enter_context(tc.tile_pool(name="held", bufs=1))
         ring = ctx.enter_context(tc.tile_pool(name="ring", bufs=8))
-        acc_banks = ctx.enter_context(tc.psum_pool(name="acc_banks", bufs=3))
-        turn_banks = ctx.enter_context(tc.psum_pool(name="turn_banks", bufs=1))
+        placed = ctx.enter_context(tc.tile_pool(name="placed", bufs=1))
+        psum = ctx.enter_context(tc.psum_pool(name="psum", bufs=1))
+
+        def bank(number, shape):
+            return psum.tile(shape, F32, name="bank%d" % number, tag="bank%d" % number)
 
         scale_table = held.tile([P, T], U8, align_bytes=64)
-        nc.vector.memset(scale_table[:].bitcast(I32), 0)
+        nc.gpsimd.memset(scale_table[:].bitcast(I32), 0)
         picks = held.tile([P, S // STRIPE], U16)
         nc.sync.dma_start(picks[:], offs)
-        w1_rows = w1.rearrange("(p j) h -> p j h", j=PACK)
-        w1_first = held.tile([P, PACK, P], F32)
         corners = [held.tile([P, V // STRIPE], U16, name="corner%d" % d) for d in range(D)]
         nc.sync.dma_start(corners[0][:], pos1)
         for r in range(4):
@@ -59,21 +51,26 @@ def tile_picked_zwarp_none_po_kernel(
             )
         word_table = held.tile([P, T], I32, align_bytes=64)
         nc.sync.dma_start(out=word_table[:], in_=x_words[0].rearrange("p c r -> p (c r)").bitcast(I32))
-        nc.sync.dma_start(out=w1_first[:], in_=w1_rows[:, :, 0:P])
-        gates = [held.tile([P, V], F32, name="gate%d" % d, tag="gate%d" % d, align_bytes=64) for d in range(D)]
+        w1_rows = w1.rearrange("(p j) h -> p j h", j=PACK)
+        w1_halves = [held.tile([P, PACK, H // 2], F32, name="w1_half%d" % h) for h in range(2)]
+        nc.sync.dma_start(out=w1_halves[0][:], in_=w1_rows[:, :, 0 : H // 2])
+        gates = [held.tile([P, V], F32, name="gate%d" % d, align_bytes=64) for d in range(D)]
+        ref_low = [held.tile([P, V], F32, name="ref_low%d" % h) for h in range(2)]
+        ref_low_rows = ref.rearrange("(h m r) v -> h m r v", h=2, r=PACK)
+        ref_high = held.tile([P, 2, V], F32)
         nc.sync.dma_start(out=gates[0][:], in_=gate[0])
-        ref_rows = ref.rearrange("(t p) v -> p t v", p=P)
-        ref_first = held.tile([P, 1, V], F32)
-        nc.sync.dma_start(out=ref_first[:], in_=ref_rows[:, 0:1, :])
-        w1_rest = held.tile([P, PACK, H - P], F32)
-        nc.sync.dma_start(out=w1_rest[:], in_=w1_rows[:, :, P:H])
-        for d, pos in ((1, pos2), (2, pos3), (3, pos4)):
+        nc.sync.dma_start(corners[1][:], pos2)
+        nc.sync.dma_start(out=gates[1][:], in_=gate[1])
+        nc.sync.dma_start(out=w1_halves[1][:], in_=w1_rows[:, :, H // 2 : H])
+        nc.sync.dma_start(out=ref_low[0][:], in_=ref_low_rows[0, :, 0:2, :])
+        for d, pos in ((2, pos3), (3, pos4)):
             nc.sync.dma_start(corners[d][:], pos)
             nc.sync.dma_start(out=gates[d][:], in_=gate[d])
-        ref_rest = held.tile([P, TILES - 1, V], F32)
-        nc.sync.dma_start(out=ref_rest[:], in_=ref_rows[:, 1:TILES, :])
+        nc.sync.dma_start(out=ref_low[1][:], in_=ref_low_rows[1, :, 0:2, :])
+        nc.sync.dma_start(out=ref_high[:], in_=ref.rearrange("(p r) v -> p r v", r=PACK)[:, 2:4, :])
         w2_raw = held.tile([P, PACK, N], F32)
         nc.sync.dma_start(out=w2_raw[:], in_=w2.rearrange("(p j) n -> p j n", j=PACK))
+        refs = [ref_low[0][:], ref_low[1][:], ref_high[:, 0, :], ref_high[:, 1, :]]
 
         identity = held.tile([P, P], F32)
         make_identity(nc, identity[:])
@@ -92,197 +89,242 @@ def tile_picked_zwarp_none_po_kernel(
             gather_words(a, b, "x_codes%d" % a)
 
         features = []
-        for t0, t1 in W1_PIECES:
-            width = (t1 - t0) * P
-            source = w1_first[:] if t0 == 0 else w1_rest[:, :, (t0 - 1) * P : (t1 - 1) * P]
-            grouped = held.tile(
-                [P, width * PACK], BF16, name="w1_grouped%d" % t0,
-                tag="w1_shared%d" % t0, align_bytes=64,
-            )
+        first_banks = [0, 1, 3, 2, 0, 1, 2, 0, 1]
+
+        def quantise(grouped, width, name, codes_tag, scales_tag):
+            codes = held.tile([P, width], U32, name=name + "_codes", tag=codes_tag, align_bytes=64)
+            scales = held.tile([P, width], U8, name=name + "_scales", tag=scales_tag, align_bytes=64)
+            nc.vector.quantize_mx(out=codes[:].bitcast(FP8X4), scales=scales[:], in_=grouped[:])
+            return codes, scales
+
+        def first_product(t, codes, scales, cols):
+            feature = held.tile([P, S], F32, name="feature%d" % t)
+            for a, b in WORD_PIECES if t == 0 else HALVES:
+                acc = bank(first_banks.pop(0), [P, b - a])
+                for pa, pb in WORD_PIECES:
+                    if a <= pa and pb <= b:
+                        nc.tensor.matmul_mx(
+                            out=acc[:, pa - a : pb - a],
+                            lhsT=codes[:, cols].bitcast(FP8X4),
+                            lhsT_scale=scales[:, cols],
+                            rhs=x_codes[pa][:].bitcast(FP8X4),
+                            rhs_scale=x_bytes[:, pa:pb],
+                            start=True,
+                            stop=True,
+                        )
+                if t == 0 and (a, b) == WORD_PIECES[1]:
+                    nc.vector.tensor_scalar_mul(feature[:, a:b], acc[:], -1.0)
+                else:
+                    nc.scalar.activation(feature[:, a:b], acc[:], COPY, scale=-1.0)
+            features.append(feature)
+
+        for h in range(2):
+            grouped = held.tile([P, P * PACK], BF16, name="w1_low%d" % h, tag="w1_shared%d" % h, align_bytes=64)
             nc.scalar.activation(
-                grouped[:].rearrange("p (c i j) -> p c j i", i=4, j=PACK),
-                source.rearrange("p j (c i) -> p c j i", i=4),
+                grouped[:].rearrange("p (m e j) -> p m j e", e=2, j=PACK),
+                w1_halves[h][:].rearrange("p j (m r) -> p m j r", r=PACK)[:, :, :, 0:2],
                 COPY,
             )
-            codes = held.tile(
-                [P, width], U32, name="w1_codes%d" % t0,
-                tag="w1_shared1" if t0 == 0 else "w1_codes%d" % t0, align_bytes=64,
+            codes, scales = quantise(
+                grouped, P, "w1_low%d" % h,
+                "w1_shared1" if h == 0 else "w1_codes1", "w1_shared2" if h == 0 else "w1_scales1",
             )
-            scales = held.tile(
-                [P, width], U8, name="w1_scales%d" % t0,
-                tag="w1_shared2" if t0 == 0 else "w1_scales%d" % t0, align_bytes=64,
-            )
-            nc.vector.quantize_mx(out=codes[:].bitcast(FP8X4), scales=scales[:], in_=grouped[:])
-            if t0 == 0:
+            if h == 0:
                 gather_words(*WORD_PIECES[-1], "w1_shared0")
-            for t in range(t0, t1):
-                cols = slice((t - t0) * P, (t - t0 + 1) * P)
-                feature = held.tile([P, S], F32, name="feature%d" % t)
-                for a, b in WORD_PIECES if t == 0 else HALVES:
-                    if t == 0 and b == S:
-                        acc = turn_banks.tile([P, b - a], F32, name="first_acc", tag="early0")
-                    else:
-                        acc = acc_banks.tile([P, b - a], F32, name="acc")
-                    for pa, pb in WORD_PIECES:
-                        if a <= pa and pb <= b:
-                            nc.tensor.matmul_mx(
-                                out=acc[:, pa - a : pb - a],
-                                lhsT=codes[:, cols].bitcast(FP8X4),
-                                lhsT_scale=scales[:, cols],
-                                rhs=x_codes[pa][:].bitcast(FP8X4),
-                                rhs_scale=x_bytes[:, pa:pb],
-                                start=True,
-                                stop=True,
-                            )
-                    if t == 0 and (a, b) == WORD_PIECES[1]:
-                        nc.vector.tensor_scalar_mul(feature[:, a:b], acc[:], -1.0)
-                    else:
-                        nc.scalar.activation(feature[:, a:b], acc[:], COPY, scale=-1.0)
-                features.append(feature)
-
+            first_product(h, codes, scales, slice(0, P))
+        grouped = held.tile([P, 2 * P * PACK], BF16, name="w1_high", tag="w1_shared2", align_bytes=64)
+        for h in range(2):
+            nc.scalar.activation(
+                grouped[:].rearrange("p (s h m j) -> p h m j s", s=2, h=2, j=PACK)[:, h],
+                w1_halves[h][:].rearrange("p j (m r) -> p m j r", r=PACK)[:, :, :, 2:4],
+                COPY,
+            )
+        codes, scales = quantise(grouped, 2 * P, "w1_high", "w1_codes2", "w1_scales2")
+        for s in range(2):
+            first_product(2 + s, codes, scales, slice(s * P, (s + 1) * P))
 
         w2_grouped = held.tile([P, N * PACK], BF16, align_bytes=64)
         nc.scalar.copy(
             w2_grouped[:].rearrange("p (t m j) -> p m j t", t=PACK, j=PACK),
             w2_raw[:].rearrange("p j (m t) -> p m j t", t=PACK),
         )
-        w2_codes = held.tile([P, N], U32, align_bytes=64)
-        w2_scales = held.tile([P, N], U8, align_bytes=64)
-        nc.vector.quantize_mx(out=w2_codes[:].bitcast(FP8X4), scales=w2_scales[:], in_=w2_grouped[:])
+        w2_codes, w2_scales = quantise(w2_grouped, N, "w2", "w2_codes", "w2_scales")
 
         out_rows = out_0.rearrange("(p t) v -> p t v", t=PACK)
         out_words = out_1[0].rearrange("p c r -> p (c r)").bitcast(I32)
         y_scales = held.tile([P, V], U8, align_bytes=64)
 
-        e_pairs = [
-            held.tile([P, (v1 - v0) // P * H], BF16, name="e_pairs%d" % v0, align_bytes=64) for v0, v1 in GROUPS
-        ]
+        def weighted(term, t, d, v0, v1):
+            nc.vector.tensor_tensor(
+                term,
+                features[t][:].indirect(corners[d][:, v0 // STRIPE : v1 // STRIPE]),
+                gates[d][:, v0:v1],
+                MULT,
+            )
 
-        late_slots = {}
-        bank_uses = []
-
-        def next_bank(shape):
-            bank_uses.append(shape)
-            return turn_banks.tile(shape, F32, name="turn", tag="turn%d" % (len(bank_uses) % 3))
-
-        def difference(t, v0, v1):
-            width = v1 - v0
-            chunks = width // P
-            ref_tile = ref_first[:, 0, :] if t == 0 else ref_rest[:, t - 1, :]
-            total = next_bank([P, chunks, P]) if t > 1 or v0 > 0 else turn_banks.tile([P, chunks, P], F32, name="early", tag="early%d" % t)
-            for c in range(chunks):
-                nc.tensor.matmul(
-                    total[:, c, :], ref_tile[:, v0 + c * P : v0 + (c + 1) * P], identity[:],
-                    is_transpose=True, start=(c == 0), stop=False,
-                )
-            for d in range(D):
-                if (t, v0, d) in HELD_BACK:
-                    g, count = HELD_BACK[(t, v0, d)]
-                    late = held.tile([P, count * P], F32, name="late_terms", tag="e_grouped%d" % g, align_bytes=64)
-                    first = GATHERS.index((t, v0, d))
-                    for n in range(count):
-                        late_slots[GATHERS[first + n]] = late[:, n * P : (n + 1) * P]
-                term = late_slots[(t, v0, d)] if (t, v0, d) in late_slots else ring.tile([P, width], F32, name="term")[:]
-                nc.vector.tensor_tensor(
-                    term,
-                    features[t][:].indirect(corners[d][:, v0 // STRIPE : v1 // STRIPE]),
-                    gates[d][:, v0:v1],
-                    MULT,
-                )
+        def turned_sum(total, tiles, v0, v1, corner_count, slots):
+            chunks = (v1 - v0) // P
+            for n, t in enumerate(tiles):
                 for c in range(chunks):
                     nc.tensor.matmul(
-                        total[:, c, :], term[:, c * P : (c + 1) * P], identity[:],
-                        is_transpose=True, start=False, stop=(d == D - 1 and c == chunks - 1),
+                        total[:, n, c, :], refs[t][:, v0 + c * P : v0 + (c + 1) * P], identity[:],
+                        is_transpose=True, start=(n == 0 and c == 0), stop=False,
                     )
-            for g, (g0, g1) in enumerate(GROUPS):
-                if v0 <= g0 and g1 <= v1:
-                    pairs = e_pairs[g][:].rearrange("v (c u p e) -> v c u p e", u=2, p=P, e=2)
-                    nc.scalar.copy(
-                        pairs[:, :, :, 32 * t : 32 * (t + 1), :],
-                        total[:, (g0 - v0) // P : (g1 - v0) // P, :].rearrange("v c (p u e) -> v c u p e", u=2, e=2),
-                    )
+            for n, t in enumerate(tiles):
+                for d in range(corner_count):
+                    term = slots.pop(0) if slots else ring.tile([P, v1 - v0], F32, name="term")[:]
+                    weighted(term, t, d, v0, v1)
+                    for c in range(chunks):
+                        nc.tensor.matmul(
+                            total[:, n, c, :], term[:, c * P : (c + 1) * P], identity[:],
+                            is_transpose=True, start=False,
+                            stop=(n == len(tiles) - 1 and d == corner_count - 1 and c == chunks - 1),
+                        )
 
-        e_planes = {}
-        results = {}
+        def second_product(acc, e_codes, e_scales, cols, out_tiles):
+            for n, t in enumerate(out_tiles):
+                nc.tensor.matmul_mx(
+                    out=acc[:, n, :],
+                    lhsT=w2_codes[:, t * P : (t + 1) * P].bitcast(FP8X4),
+                    lhsT_scale=w2_scales[:, t * P : (t + 1) * P],
+                    rhs=e_codes[:, cols].bitcast(FP8X4),
+                    rhs_scale=e_scales[:, cols],
+                    start=True,
+                    stop=True,
+                )
 
-        def turn_back(g):
-            v0, v1 = GROUPS[g]
-            width = v1 - v0
-            chunks = width // P
-            e_words = e_pairs[g][:].bitcast(F32)
-            back = next_bank([P, chunks, 2, P])
-            for c in range(chunks):
-                for u in range(2):
-                    nc.tensor.transpose(back[:, c, u, :], e_words[:, (2 * c + u) * P : (2 * c + u + 1) * P], identity[:])
-            e_grouped = held.tile([P, width * PACK], BF16, name="e_grouped", tag="e_grouped%d" % g, align_bytes=64)
+        early_pairs = held.tile([P, 2 * H], BF16, align_bytes=64)
+        early_view = early_pairs[:].rearrange("v (c u q) -> v c u q", u=2, q=2 * P)
+        late_pairs = held.tile([P, H], BF16, align_bytes=64)
+        late_view = late_pairs[:].rearrange("v (c q) -> v c q", q=2 * P)
+
+        total = bank(3, [P, 1, 4, P])
+        turned_sum(total, (0,), 0, V, D, [])
+        nc.scalar.copy(early_view[:, :, 0, 0:P], total[:, 0, 0:2, :])
+        nc.scalar.copy(late_view[:, :, 0:P], total[:, 0, 2:4, :])
+        total = bank(4, [P, 1, 2, P])
+        turned_sum(total, (1,), 0, EARLY, D, [])
+        nc.scalar.copy(early_view[:, :, 0, P : 2 * P], total[:, 0, :, :])
+        total = bank(5, [P, 2, 2, P])
+        turned_sum(total, (2, 3), 0, EARLY, D, [])
+        nc.scalar.copy(
+            early_view[:, :, 1, :].rearrange("v c (p s) -> v c p s", s=2),
+            total[:].rearrange("v s c p -> v c p s"),
+        )
+        early_words = early_pairs[:].bitcast(F32)
+        back = bank(6, [P, 2, 2, P])
+        for c in range(2):
+            for u in range(2):
+                nc.tensor.transpose(back[:, c, u, :], early_words[:, (2 * c + u) * P : (2 * c + u + 1) * P], identity[:])
+        early_grouped = [
+            held.tile([P, P * PACK], BF16, name="early_grouped%d" % c, tag="early_shared%d" % c, align_bytes=64)
+            for c in range(2)
+        ]
+        for c in range(2):
             nc.scalar.copy(
-                e_grouped[:].bitcast(F32).rearrange("p (c v u) -> p c v u", v=P, u=2),
-                back[:].rearrange("p c u v -> p c v u"),
+                early_grouped[c][:].bitcast(F32).rearrange("p (v u) -> p v u", u=2),
+                back[:, c].rearrange("p u v -> p v u"),
             )
-            e_codes = held.tile(
-                [P, width], U32, name="e_codes%d" % g, tag="gate%d" % (D - 1) if g == 1 else "e_codes%d" % g, align_bytes=64
+        total = bank(5, [P, 1, 2, P])
+        turned_sum(total, (1,), EARLY, V, D, [])
+        nc.scalar.copy(late_view[:, :, P : 2 * P], total[:, 0, :, :])
+
+        early_planes = [
+            quantise(early_grouped[c], P, "e_early%d" % c, "e_early_codes%d" % c, "e_early_scales%d" % c) for c in range(2)
+        ]
+        late_terms = held.tile([P, 16 * P], F32, name="late_terms", tag="early_shared0", align_bytes=64)
+        slots = [late_terms[:, n * P : (n + 1) * P] for n in range(12)]
+        y_early = held.tile([P, PACK, EARLY], F32)
+        for c in range(2):
+            acc = bank(c, [P, PACK, P])
+            second_product(acc, *early_planes[c], slice(0, P), range(PACK))
+            nc.scalar.copy(y_early[:, :, c * P : (c + 1) * P], acc[:])
+        nc.sync.dma_start(out=out_rows[:, :, 0:EARLY], in_=y_early[:])
+
+        late_words = late_pairs[:].bitcast(F32)
+        back = bank(3, [P, 2, P])
+        for c in range(2):
+            nc.tensor.transpose(back[:, c, :], late_words[:, c * P : (c + 1) * P], identity[:])
+        late_grouped = [
+            held.tile([P, P * PACK], BF16, name="late_grouped0", align_bytes=64),
+            held.tile([P, P * PACK], BF16, name="late_grouped1", tag="late_shared1", align_bytes=64),
+        ]
+        for c in range(2):
+            nc.scalar.copy(late_grouped[c][:].bitcast(F32).rearrange("p (v u) -> p v u", u=2)[:, :, 0], back[:, c, :])
+
+
+        partials = []
+        turned = [
+            held.tile([P, 2 * P], F32, name="turned0")[:],
+            placed.tile([P, 2 * P], F32, name="turned1", align_bytes=64, offset=0)[:],
+        ]
+        for c, parts in enumerate(((((2, 3), 4),), (((2,), 7), ((3,), 2)))):
+            v0 = EARLY + c * P
+            partial = bank((6, 5)[c], [P, 2, P])
+            for tiles, number in parts:
+                total = bank(number, [P, len(tiles), 1, P])
+                turned_sum(total, tiles, v0, v0 + P, D - 1, slots)
+                s0, s1 = tiles[0] - 2, tiles[-1] - 1
+                nc.scalar.copy(turned[c][:, s0 * P : s1 * P], total[:].rearrange("v s c p -> v (s c p)"))
+                for s in range(s0, s1):
+                    nc.tensor.transpose(partial[:, s, :], turned[c][:, s * P : (s + 1) * P], identity[:])
+            partials.append(partial)
+
+        y_grouped = held.tile([P, EARLY * PACK], BF16, name="y_early_grouped", align_bytes=64)
+        nc.scalar.copy(
+            y_grouped[:].rearrange("p (c i t) -> p c t i", i=4, t=PACK),
+            y_early[:].rearrange("p t (c i) -> p c t i", i=4),
+        )
+
+        for c in range(2):
+            for s in range(2):
+                n = 12 + 2 * c + s
+                weighted(late_terms[:, n * P : (n + 1) * P], 2 + s, D - 1, EARLY + c * P, EARLY + (c + 1) * P)
+        for c in range(2):
+            nc.vector.tensor_tensor(
+                late_grouped[c][:].rearrange("p (v j) -> p v j", j=PACK)[:, :, 2:4],
+                late_terms[:, (12 + 2 * c) * P : (14 + 2 * c) * P].rearrange("p (s v) -> p v s", s=2),
+                partials[c][:].rearrange("p s v -> p v s"),
+                ADD,
             )
-            e_scales = held.tile([P, width], U8, name="e_scales%d" % g, align_bytes=64)
-            nc.vector.quantize_mx(out=e_codes[:].bitcast(FP8X4), scales=e_scales[:], in_=e_grouped[:])
-            e_planes[g] = (e_codes, e_scales)
-            results[g] = held.tile([P, PACK, width], F32, name="y%d" % v0)
+        late_e_codes = [
+            placed.tile([P, P], U32, name="late_e_codes0", align_bytes=64, offset=0),
+            held.tile([P, P], U32, name="late_e_codes1", align_bytes=64),
+        ]
+        late_e_scales = [held.tile([P, P], U8, name="late_e_scales%d" % c, align_bytes=64) for c in range(2)]
+        for c in range(2):
+            nc.vector.quantize_mx(
+                out=late_e_codes[c][:].bitcast(FP8X4), scales=late_e_scales[c][:], in_=late_grouped[c][:]
+            )
 
-        def second_product(g, c):
-            v0, v1 = GROUPS[g]
-            last = v1 == V
-            e_codes, e_scales = e_planes[g]
-            y = results[g]
-            cols = slice(c * P, (c + 1) * P)
-            per_bank = PACK // 2 if last else PACK
-            for t0 in range(0, PACK, per_bank):
-                acc = acc_banks.tile([P, per_bank, P], F32, name="acc") if g == 0 else next_bank([P, per_bank, P])
-                for t in range(t0, t0 + per_bank):
-                    nc.tensor.matmul_mx(
-                        out=acc[:, t - t0, :],
-                        lhsT=w2_codes[:, t * P : (t + 1) * P].bitcast(FP8X4),
-                        lhsT_scale=w2_scales[:, t * P : (t + 1) * P],
-                        rhs=e_codes[:, cols].bitcast(FP8X4),
-                        rhs_scale=e_scales[:, cols],
-                        start=True,
-                        stop=True,
-                    )
-                nc.scalar.copy(y[:, t0 : t0 + per_bank, cols], acc[:])
-            if v0 + (c + 1) * P == v1:
-                (nc.scalar if last else nc.sync).dma_start(out=out_rows[:, :, v0:v1], in_=y[:])
+        y_codes = held.tile([P, EARLY], I32, name="y_early_codes", tag="late_shared1", align_bytes=64)
+        nc.vector.quantize_mx(out=y_codes[:].bitcast(FP8X4), scales=y_scales[:, 0:EARLY], in_=y_grouped[:])
+        nc.sync.dma_start(out=out_words[:, 0:EARLY], in_=y_codes[:])
 
-        def early_planes(g):
-            v0, v1 = GROUPS[g]
-            width = v1 - v0
-            y_grouped = held.tile([P, width * PACK], BF16, name="early_grouped", tag="e_grouped%d" % g, align_bytes=64)
-            y_codes = held.tile([P, width], I32, name="early_codes%d" % g, align_bytes=64)
+        late_codes = held.tile([P, V - EARLY], I32, align_bytes=64)
+        y_late_grouped = [held.tile([P, P * PACK], BF16, name="y_late_grouped%d" % c, align_bytes=64) for c in range(2)]
+        for c in range(2):
+            v0 = EARLY + c * P
+            y_late = held.tile([P, PACK, P], F32, name="y_late%d" % c)
+            for h in range(2):
+                acc = bank(((2, 4), (0, 1))[c][h], [P, 2, P])
+                second_product(acc, late_e_codes[c], late_e_scales[c], slice(0, P), range(2 * h, 2 * h + 2))
+                emptying = nc.vector.tensor_copy if (c, h) == (0, 1) else nc.scalar.copy
+                emptying(y_late[:, 2 * h : 2 * h + 2, :], acc[:])
+            (nc.sync if c == 0 else nc.scalar).dma_start(out=out_rows[:, :, v0 : v0 + P], in_=y_late[:])
             nc.vector.tensor_copy(
-                y_grouped[:].rearrange("p (c i t) -> p c t i", i=4, t=PACK),
-                results[g][:].rearrange("p t (c i) -> p c t i", i=4),
+                y_late_grouped[c][:].rearrange("p (c i t) -> p c t i", i=4, t=PACK),
+                y_late[:].rearrange("p t (c i) -> p c t i", i=4),
             )
-            nc.vector.quantize_mx(out=y_codes[:].bitcast(FP8X4), scales=y_scales[:, v0:v1], in_=y_grouped[:])
-            nc.sync.dma_start(out=out_words[:, v0:v1], in_=y_codes[:])
-
-        difference(0, 0, 512)
-        difference(1, 0, 384)
-        difference(2, 0, 256)
-        difference(3, 0, 256)
-        difference(2, 256, 512)
-        turn_back(0)
-        difference(3, 256, 384)
-        difference(1, 384, 512)
-        turn_back(1)
-        second_product(0, 0)
-        second_product(0, 1)
-        difference(3, 384, 512)
-        second_product(1, 0)
-        early_planes(0)
-        turn_back(2)
-        early_planes(1)
-        second_product(2, 0)
-        early_planes(2)
-
-        for q in range(4):
-            (nc.sync if q < 2 else nc.scalar).dma_start(
-                out=out_2[0, 4 * q : 4 * q + 4, :].bitcast(I32),
-                in_=y_scales[32 * q : 32 * q + 4, :].bitcast(I32),
+        for c in range(2):
+            v0 = EARLY + c * P
+            nc.vector.quantize_mx(
+                out=late_codes[:, c * P : (c + 1) * P].bitcast(FP8X4), scales=y_scales[:, v0 : v0 + P],
+                in_=y_late_grouped[c][:],
+            )
+        nc.sync.dma_start(out=out_words[:, EARLY:V], in_=late_codes[:])
+        for r in range(4):
+            (nc.sync if r < 2 else nc.scalar).dma_start(
+                out=out_2[0, r:16:4, :].bitcast(I32),
+                in_=y_scales[r:P:32, :].bitcast(I32),
             )

@@ -193,6 +193,12 @@ def tile_picked_zwarp_none_po_kernel(
                     stop=True,
                 )
 
+        def round_for_planes(copy, grouped, y):
+            copy(
+                grouped[:].rearrange("p (c i t) -> p c t i", i=4, t=PACK),
+                y.rearrange("p t (c i) -> p c t i", i=4),
+            )
+
         early_pairs = held.tile([P, 2 * H], BF16, align_bytes=64)
         early_view = early_pairs[:].rearrange("v (c u q) -> v c u q", u=2, q=2 * P)
         late_pairs = held.tile([P, H], BF16, align_bytes=64)
@@ -205,17 +211,22 @@ def tile_picked_zwarp_none_po_kernel(
         total = bank(4, [P, 1, 2, P])
         turned_sum(total, (1,), 0, EARLY, D, [])
         nc.scalar.copy(early_view[:, :, 0, P : 2 * P], total[:, 0, :, :])
+        early_words = early_pairs[:].bitcast(F32)
+        backs = [bank(6 + c, [P, 2, P]) for c in range(2)]
+
+        def turn_back_early(c, u):
+            nc.tensor.transpose(backs[c][:, u, :], early_words[:, (2 * c + u) * P : (2 * c + u + 1) * P], identity[:])
+
+        for c in range(2):
+            turn_back_early(c, 0)
         total = bank(5, [P, 2, 2, P])
         turned_sum(total, (2, 3), 0, EARLY, D, [])
-        nc.scalar.copy(
-            early_view[:, :, 1, :].rearrange("v c (p s) -> v c p s", s=2),
-            total[:].rearrange("v s c p -> v c p s"),
-        )
-        early_words = early_pairs[:].bitcast(F32)
-        back = bank(6, [P, 2, 2, P])
         for c in range(2):
-            for u in range(2):
-                nc.tensor.transpose(back[:, c, u, :], early_words[:, (2 * c + u) * P : (2 * c + u + 1) * P], identity[:])
+            nc.scalar.copy(
+                early_view[:, c, 1, :].rearrange("v (p s) -> v p s", s=2),
+                total[:, :, c, :].rearrange("v s p -> v p s"),
+            )
+            turn_back_early(c, 1)
         early_grouped = [
             held.tile([P, P * PACK], BF16, name="early_grouped%d" % c, tag="early_shared%d" % c, align_bytes=64)
             for c in range(2)
@@ -223,7 +234,7 @@ def tile_picked_zwarp_none_po_kernel(
         for c in range(2):
             nc.scalar.copy(
                 early_grouped[c][:].bitcast(F32).rearrange("p (v u) -> p v u", u=2),
-                back[:, c].rearrange("p u v -> p v u"),
+                backs[c][:].rearrange("p u v -> p v u"),
             )
         total = bank(5, [P, 1, 2, P])
         turned_sum(total, (1,), EARLY, V, D, [])
@@ -239,6 +250,9 @@ def tile_picked_zwarp_none_po_kernel(
             acc = bank(c, [P, PACK, P])
             second_product(acc, *early_planes[c], slice(0, P), range(PACK))
             nc.scalar.copy(y_early[:, :, c * P : (c + 1) * P], acc[:])
+            if c == 0:
+                first_grouped = held.tile([P, P * PACK], BF16, align_bytes=64)
+                round_for_planes(nc.scalar.copy, first_grouped, y_early[:, :, 0:P])
         nc.sync.dma_start(out=out_rows[:, :, 0:EARLY], in_=y_early[:])
 
         late_words = late_pairs[:].bitcast(F32)
@@ -247,7 +261,7 @@ def tile_picked_zwarp_none_po_kernel(
             nc.tensor.transpose(back[:, c, :], late_words[:, c * P : (c + 1) * P], identity[:])
         late_grouped = [
             held.tile([P, P * PACK], BF16, name="late_grouped0", align_bytes=64),
-            held.tile([P, P * PACK], BF16, name="late_grouped1", tag="late_shared1", align_bytes=64),
+            placed.tile([P, P * PACK], BF16, name="late_grouped1", align_bytes=64, offset=2048),
         ]
         for c in range(2):
             nc.scalar.copy(late_grouped[c][:].bitcast(F32).rearrange("p (v u) -> p v u", u=2)[:, :, 0], back[:, c, :])
@@ -270,11 +284,6 @@ def tile_picked_zwarp_none_po_kernel(
                     nc.tensor.transpose(partial[:, s, :], turned[c][:, s * P : (s + 1) * P], identity[:])
             partials.append(partial)
 
-        y_grouped = held.tile([P, EARLY * PACK], BF16, name="y_early_grouped", align_bytes=64)
-        nc.scalar.copy(
-            y_grouped[:].rearrange("p (c i t) -> p c t i", i=4, t=PACK),
-            y_early[:].rearrange("p t (c i) -> p c t i", i=4),
-        )
 
         for c in range(2):
             for s in range(2):
@@ -297,8 +306,13 @@ def tile_picked_zwarp_none_po_kernel(
                 out=late_e_codes[c][:].bitcast(FP8X4), scales=late_e_scales[c][:], in_=late_grouped[c][:]
             )
 
-        y_codes = held.tile([P, EARLY], I32, name="y_early_codes", tag="late_shared1", align_bytes=64)
-        nc.vector.quantize_mx(out=y_codes[:].bitcast(FP8X4), scales=y_scales[:, 0:EARLY], in_=y_grouped[:])
+        second_grouped = placed.tile([P, P * PACK], BF16, name="second_grouped", align_bytes=64, offset=2560)
+        round_for_planes(nc.vector.tensor_copy, second_grouped, y_early[:, :, P:EARLY])
+        y_codes = placed.tile([P, EARLY], I32, name="y_early_codes", align_bytes=64, offset=1536)
+        for c, grouped in enumerate((first_grouped, second_grouped)):
+            nc.vector.quantize_mx(
+                out=y_codes[:, c * P : (c + 1) * P].bitcast(FP8X4), scales=y_scales[:, c * P : (c + 1) * P], in_=grouped[:]
+            )
         nc.sync.dma_start(out=out_words[:, 0:EARLY], in_=y_codes[:])
 
         late_codes = held.tile([P, V - EARLY], I32, align_bytes=64)
@@ -312,10 +326,7 @@ def tile_picked_zwarp_none_po_kernel(
                 emptying = nc.vector.tensor_copy if (c, h) == (0, 1) else nc.scalar.copy
                 emptying(y_late[:, 2 * h : 2 * h + 2, :], acc[:])
             (nc.sync if c == 0 else nc.scalar).dma_start(out=out_rows[:, :, v0 : v0 + P], in_=y_late[:])
-            nc.vector.tensor_copy(
-                y_late_grouped[c][:].rearrange("p (c i t) -> p c t i", i=4, t=PACK),
-                y_late[:].rearrange("p t (c i) -> p c t i", i=4),
-            )
+            round_for_planes(nc.vector.tensor_copy, y_late_grouped[c], y_late[:])
         for c in range(2):
             v0 = EARLY + c * P
             nc.vector.quantize_mx(

@@ -22,6 +22,7 @@ PACK = 4
 STRIPE = 16
 EARLY = 256
 WORD_PIECES = ((0, 512), (512, 768), (768, 1024))
+FIRST_PIECES = ((0, 512), (512, 768), (768, 896), (896, 1024))
 HALVES = ((0, 512), (512, 1024))
 
 
@@ -58,10 +59,10 @@ def tile_picked_zwarp_none_po_kernel(
         ref_low = [held.tile([P, V], F32, name="ref_low%d" % h) for h in range(2)]
         ref_low_rows = ref.rearrange("(h m r) v -> h m r v", h=2, r=PACK)
         ref_high = held.tile([P, 2, V], F32)
+        nc.sync.dma_start(out=w1_halves[1][:], in_=w1_rows[:, :, H // 2 : H])
         nc.sync.dma_start(out=gates[0][:], in_=gate[0])
         nc.sync.dma_start(corners[1][:], pos2)
         nc.sync.dma_start(out=gates[1][:], in_=gate[1])
-        nc.sync.dma_start(out=w1_halves[1][:], in_=w1_rows[:, :, H // 2 : H])
         nc.sync.dma_start(out=ref_low[0][:], in_=ref_low_rows[0, :, 0:2, :])
         for d, pos in ((2, pos3), (3, pos4)):
             nc.sync.dma_start(corners[d][:], pos)
@@ -89,7 +90,7 @@ def tile_picked_zwarp_none_po_kernel(
             gather_words(a, b, "x_codes%d" % a)
 
         features = []
-        first_banks = [0, 1, 3, 2, 0, 1, 2, 0, 1]
+        first_banks = [0, 1, 4, 3, 2, 0, 1, 2, 0, 1]
 
         def quantise(grouped, width, name, codes_tag, scales_tag):
             codes = held.tile([P, width], U32, name=name + "_codes", tag=codes_tag, align_bytes=64)
@@ -99,20 +100,21 @@ def tile_picked_zwarp_none_po_kernel(
 
         def first_product(t, codes, scales, cols):
             feature = held.tile([P, S], F32, name="feature%d" % t)
-            for a, b in WORD_PIECES if t == 0 else HALVES:
+            for a, b in FIRST_PIECES if t == 0 else HALVES:
                 acc = bank(first_banks.pop(0), [P, b - a])
                 for pa, pb in WORD_PIECES:
-                    if a <= pa and pb <= b:
+                    lo, hi = max(a, pa), min(b, pb)
+                    if lo < hi:
                         nc.tensor.matmul_mx(
-                            out=acc[:, pa - a : pb - a],
+                            out=acc[:, lo - a : hi - a],
                             lhsT=codes[:, cols].bitcast(FP8X4),
                             lhsT_scale=scales[:, cols],
-                            rhs=x_codes[pa][:].bitcast(FP8X4),
-                            rhs_scale=x_bytes[:, pa:pb],
+                            rhs=x_codes[pa][:, lo - pa : hi - pa].bitcast(FP8X4),
+                            rhs_scale=x_bytes[:, lo:hi],
                             start=True,
                             stop=True,
                         )
-                if t == 0 and (a, b) == WORD_PIECES[1]:
+                if t == 0 and (a, b) in FIRST_PIECES[1:3]:
                     nc.vector.tensor_scalar_mul(feature[:, a:b], acc[:], -1.0)
                 else:
                     nc.scalar.activation(feature[:, a:b], acc[:], COPY, scale=-1.0)
@@ -127,7 +129,7 @@ def tile_picked_zwarp_none_po_kernel(
             )
             codes, scales = quantise(
                 grouped, P, "w1_low%d" % h,
-                "w1_shared1" if h == 0 else "w1_codes1", "w1_shared2" if h == 0 else "w1_scales1",
+                "w1_codes%d" % h, "w1_shared2" if h == 0 else "w1_scales1",
             )
             if h == 0:
                 gather_words(*WORD_PIECES[-1], "w1_shared0")
@@ -220,7 +222,32 @@ def tile_picked_zwarp_none_po_kernel(
         for c in range(2):
             turn_back_early(c, 0)
         total = bank(5, [P, 2, 2, P])
-        turned_sum(total, (2, 3), 0, EARLY, D, [])
+        first_late = bank(2, [P, P])
+        for n, t in enumerate((2, 3)):
+            for c in range(2):
+                nc.tensor.matmul(
+                    total[:, n, c, :], refs[t][:, c * P : (c + 1) * P], identity[:],
+                    is_transpose=True, start=(n == 0 and c == 0), stop=False,
+                )
+        nc.tensor.matmul(first_late[:], refs[3][:, EARLY : EARLY + P], identity[:], is_transpose=True, start=True, stop=False)
+        for n, t in enumerate((2, 3)):
+            for d in range(D):
+                wide = t == 3 and d < D - 1
+                width = EARLY + P if wide else EARLY
+                term = ring.tile([P, width], F32, name="term")
+                weighted(term[:], t, d, 0, width)
+                for c in range(2):
+                    nc.tensor.matmul(
+                        total[:, n, c, :], term[:, c * P : (c + 1) * P], identity[:],
+                        is_transpose=True, start=False, stop=(t == 3 and d == D - 1 and c == 1),
+                    )
+                if wide:
+                    nc.tensor.matmul(
+                        first_late[:], term[:, EARLY : EARLY + P], identity[:],
+                        is_transpose=True, start=False, stop=(d == D - 2),
+                    )
+        turned3 = held.tile([P, P], F32)
+        nc.scalar.copy(turned3[:], first_late[:])
         for c in range(2):
             nc.scalar.copy(
                 early_view[:, c, 1, :].rearrange("v (p s) -> v p s", s=2),
@@ -244,15 +271,12 @@ def tile_picked_zwarp_none_po_kernel(
             quantise(early_grouped[c], P, "e_early%d" % c, "e_early_codes%d" % c, "e_early_scales%d" % c) for c in range(2)
         ]
         late_terms = held.tile([P, 16 * P], F32, name="late_terms", tag="early_shared0", align_bytes=64)
-        slots = [late_terms[:, n * P : (n + 1) * P] for n in range(12)]
+        slots = [late_terms[:, n * P : (n + 2) * P] for n in (0, 2, 4)] + [late_terms[:, n * P : (n + 1) * P] for n in range(6, 9)]
         y_early = held.tile([P, PACK, EARLY], F32)
         for c in range(2):
             acc = bank(c, [P, PACK, P])
             second_product(acc, *early_planes[c], slice(0, P), range(PACK))
             nc.scalar.copy(y_early[:, :, c * P : (c + 1) * P], acc[:])
-            if c == 0:
-                first_grouped = held.tile([P, P * PACK], BF16, align_bytes=64)
-                round_for_planes(nc.scalar.copy, first_grouped, y_early[:, :, 0:P])
         nc.sync.dma_start(out=out_rows[:, :, 0:EARLY], in_=y_early[:])
 
         late_words = late_pairs[:].bitcast(F32)
@@ -264,40 +288,41 @@ def tile_picked_zwarp_none_po_kernel(
             placed.tile([P, P * PACK], BF16, name="late_grouped1", align_bytes=64, offset=2048),
         ]
         for c in range(2):
-            nc.scalar.copy(late_grouped[c][:].bitcast(F32).rearrange("p (v u) -> p v u", u=2)[:, :, 0], back[:, c, :])
+            nc.scalar.copy(
+                late_grouped[c][:].bitcast(F32).rearrange("p (v u) -> p v u", u=2),
+                back[:, c, :].unsqueeze(2).to_broadcast([P, P, 2]),
+            )
 
 
-        partials = []
+        partials = [bank(number, [P, 2, P]) for number in (6, 5)]
         turned = [
-            held.tile([P, 2 * P], F32, name="turned0")[:],
-            placed.tile([P, 2 * P], F32, name="turned1", align_bytes=64, offset=0)[:],
+            held.tile([P, 2 * P], F32, name="turned2")[:],
+            placed.tile([P, P], F32, name="turned_last", align_bytes=64, offset=4608)[:],
         ]
-        for c, parts in enumerate(((((2, 3), 4),), (((2,), 7), ((3,), 2)))):
-            v0 = EARLY + c * P
-            partial = bank((6, 5)[c], [P, 2, P])
-            for tiles, number in parts:
-                total = bank(number, [P, len(tiles), 1, P])
-                turned_sum(total, tiles, v0, v0 + P, D - 1, slots)
-                s0, s1 = tiles[0] - 2, tiles[-1] - 1
-                nc.scalar.copy(turned[c][:, s0 * P : s1 * P], total[:].rearrange("v s c p -> v (s c p)"))
-                for s in range(s0, s1):
-                    nc.tensor.transpose(partial[:, s, :], turned[c][:, s * P : (s + 1) * P], identity[:])
-            partials.append(partial)
+        nc.tensor.transpose(partials[0][:, 1, :], turned3[:], identity[:])
+        parts = ((2, 0, 2, 4), (3, 1, 2, 7))
+        for (t, c0, c1, number), sums in zip(parts, turned):
+            total = bank(number, [P, 1, c1 - c0, P])
+            turned_sum(total, (t,), EARLY + c0 * P, EARLY + c1 * P, D - 1, slots)
+            nc.scalar.copy(sums, total[:].rearrange("v s c p -> v (s c p)"))
+            for c in range(c0, c1):
+                nc.tensor.transpose(partials[c][:, t - 2, :], sums[:, (c - c0) * P : (c - c0 + 1) * P], identity[:])
 
-
+        first_grouped = placed.tile([P, P * PACK], BF16, name="first_grouped", align_bytes=64, offset=4864)
+        round_for_planes(nc.scalar.copy, first_grouped, y_early[:, :, 0:P])
+        weighted(late_terms[:, 12 * P : 14 * P], 2, D - 1, EARLY, V)
         for c in range(2):
-            for s in range(2):
-                n = 12 + 2 * c + s
-                weighted(late_terms[:, n * P : (n + 1) * P], 2 + s, D - 1, EARLY + c * P, EARLY + (c + 1) * P)
+            weighted(late_terms[:, (14 + c) * P : (15 + c) * P], 3, D - 1, EARLY + c * P, EARLY + (c + 1) * P)
+        last_terms = late_terms[:, 12 * P : 16 * P].rearrange("p (s c v) -> p c v s", s=2, c=2)
         for c in range(2):
             nc.vector.tensor_tensor(
                 late_grouped[c][:].rearrange("p (v j) -> p v j", j=PACK)[:, :, 2:4],
-                late_terms[:, (12 + 2 * c) * P : (14 + 2 * c) * P].rearrange("p (s v) -> p v s", s=2),
+                last_terms[:, c],
                 partials[c][:].rearrange("p s v -> p v s"),
                 ADD,
             )
         late_e_codes = [
-            placed.tile([P, P], U32, name="late_e_codes0", align_bytes=64, offset=0),
+            placed.tile([P, P], U32, name="late_e_codes0", align_bytes=64, offset=4352),
             held.tile([P, P], U32, name="late_e_codes1", align_bytes=64),
         ]
         late_e_scales = [held.tile([P, P], U8, name="late_e_scales%d" % c, align_bytes=64) for c in range(2)]
@@ -321,7 +346,7 @@ def tile_picked_zwarp_none_po_kernel(
             v0 = EARLY + c * P
             y_late = held.tile([P, PACK, P], F32, name="y_late%d" % c)
             for h in range(2):
-                acc = bank(((2, 4), (0, 1))[c][h], [P, 2, P])
+                acc = bank(((7, 4), (0, 1))[c][h], [P, 2, P])
                 second_product(acc, late_e_codes[c], late_e_scales[c], slice(0, P), range(2 * h, 2 * h + 2))
                 emptying = nc.vector.tensor_copy if (c, h) == (0, 1) else nc.scalar.copy
                 emptying(y_late[:, 2 * h : 2 * h + 2, :], acc[:])

@@ -80,17 +80,17 @@ def tile_picked_zwarp_none_po_kernel(
         nc.vector.tensor_copy(x_bytes[:], scale_table[:].indirect(picks[:]))
         x_codes = {}
 
-        def gather_words(a, b, tag):
-            x_codes[a] = held.tile([P, b - a], U32, name="x_codes%d" % a, tag=tag, align_bytes=64)
+        def gather_words(a, b, tile):
+            x_codes[a] = tile
             nc.vector.tensor_copy(
                 x_codes[a][:], word_table[:].bitcast(U32).indirect(picks[:, a // STRIPE : b // STRIPE])
             )
 
         for a, b in WORD_PIECES[:-1]:
-            gather_words(a, b, "x_codes%d" % a)
+            gather_words(a, b, held.tile([P, b - a], U32, name="x_codes%d" % a, align_bytes=64))
 
         features = []
-        first_banks = [0, 1, 4, 3, 2, 0, 1, 2, 0, 1]
+        first_banks = [0, 1, 4, 3, 2, 5, 6, 7, 0, 1]
 
         def quantise(grouped, width, name, codes_tag, scales_tag):
             codes = held.tile([P, width], U32, name=name + "_codes", tag=codes_tag, align_bytes=64)
@@ -114,55 +114,60 @@ def tile_picked_zwarp_none_po_kernel(
                             start=True,
                             stop=True,
                         )
-                if t == 0 and (a, b) in FIRST_PIECES[1:3]:
+                if t == 0 and (a, b) in FIRST_PIECES[2:3]:
                     nc.vector.tensor_scalar_mul(feature[:, a:b], acc[:], -1.0)
                 else:
                     nc.scalar.activation(feature[:, a:b], acc[:], COPY, scale=-1.0)
             features.append(feature)
 
-        for h in range(2):
-            grouped = held.tile([P, P * PACK], BF16, name="w1_low%d" % h, tag="w1_shared%d" % h, align_bytes=64)
-            nc.scalar.activation(
-                grouped[:].rearrange("p (m e j) -> p m j e", e=2, j=PACK),
+        low_grouped = [
+            placed.tile([P, P * PACK], BF16, name="w1_low%d" % h, align_bytes=64, offset=8704 - 512 * h) for h in range(2)
+        ]
+        high_grouped = held.tile([P, 2 * P * PACK], BF16, align_bytes=64)
+
+        def round_low(copy, h):
+            copy(
+                low_grouped[h][:].rearrange("p (m e j) -> p m j e", e=2, j=PACK),
                 w1_halves[h][:].rearrange("p j (m r) -> p m j r", r=PACK)[:, :, :, 0:2],
-                COPY,
             )
-            codes, scales = quantise(
-                grouped, P, "w1_low%d" % h,
-                "w1_codes%d" % h, "w1_shared2" if h == 0 else "w1_scales1",
-            )
-            if h == 0:
-                gather_words(*WORD_PIECES[-1], "w1_shared0")
-            first_product(h, codes, scales, slice(0, P))
-        grouped = held.tile([P, 2 * P * PACK], BF16, name="w1_high", tag="w1_shared2", align_bytes=64)
-        for h in range(2):
-            nc.scalar.activation(
-                grouped[:].rearrange("p (s h m j) -> p h m j s", s=2, h=2, j=PACK)[:, h],
+
+        def round_high(h):
+            nc.scalar.copy(
+                high_grouped[:].rearrange("p (s h m j) -> p h m j s", s=2, h=2, j=PACK)[:, h],
                 w1_halves[h][:].rearrange("p j (m r) -> p m j r", r=PACK)[:, :, :, 2:4],
-                COPY,
             )
-        codes, scales = quantise(grouped, 2 * P, "w1_high", "w1_codes2", "w1_scales2")
+
+        round_low(nc.scalar.copy, 0)
+        round_high(0)
+        round_high(1)
+        codes, scales = quantise(low_grouped[0], P, "w1_low0", "w1_codes0", "w1_scales0")
+        gather_words(*WORD_PIECES[-1], placed.tile([P, 256], U32, name="x_codes_last", align_bytes=64, offset=9216))
+        first_product(0, codes, scales, slice(0, P))
+        round_low(nc.vector.tensor_copy, 1)
+        codes, scales = quantise(low_grouped[1], P, "w1_low1", "w1_codes1", "w1_scales1")
+        first_product(1, codes, scales, slice(0, P))
+        codes, scales = quantise(high_grouped, 2 * P, "w1_high", "w1_codes2", "w1_scales2")
         for s in range(2):
             first_product(2 + s, codes, scales, slice(s * P, (s + 1) * P))
-
-        w2_grouped = held.tile([P, N * PACK], BF16, align_bytes=64)
-        nc.scalar.copy(
-            w2_grouped[:].rearrange("p (t m j) -> p m j t", t=PACK, j=PACK),
-            w2_raw[:].rearrange("p j (m t) -> p m j t", t=PACK),
-        )
-        w2_codes, w2_scales = quantise(w2_grouped, N, "w2", "w2_codes", "w2_scales")
 
         out_rows = out_0.rearrange("(p t) v -> p t v", t=PACK)
         out_words = out_1[0].rearrange("p c r -> p (c r)").bitcast(I32)
         y_scales = held.tile([P, V], U8, align_bytes=64)
 
+        looked = {}
+
+        def fetched(t, d, v0, v1):
+            return features[t][:].indirect(corners[d][:, v0 // STRIPE : v1 // STRIPE])
+
+        def look_ahead(t, d, v0, v1, into=None):
+            if into is None:
+                into = held.tile([P, v1 - v0], F32, name="looked%d_%d_%d" % (t, d, v0))[:]
+            looked[t, d, v0] = into
+            nc.scalar.activation(into, fetched(t, d, v0, v1), COPY)
+
         def weighted(term, t, d, v0, v1):
-            nc.vector.tensor_tensor(
-                term,
-                features[t][:].indirect(corners[d][:, v0 // STRIPE : v1 // STRIPE]),
-                gates[d][:, v0:v1],
-                MULT,
-            )
+            values = looked[t, d, v0] if (t, d, v0) in looked else fetched(t, d, v0, v1)
+            nc.vector.tensor_tensor(term, values, gates[d][:, v0:v1], MULT)
 
         def turned_sum(total, tiles, v0, v1, corner_count, slots):
             chunks = (v1 - v0) // P
@@ -201,17 +206,23 @@ def tile_picked_zwarp_none_po_kernel(
                 y.rearrange("p t (c i) -> p c t i", i=4),
             )
 
-        early_pairs = held.tile([P, 2 * H], BF16, align_bytes=64)
+        early_pairs = held.tile([P, 2 * H], BF16, name="early_pairs", tag="early_pairs", align_bytes=64)
         early_view = early_pairs[:].rearrange("v (c u q) -> v c u q", u=2, q=2 * P)
         late_pairs = held.tile([P, H], BF16, align_bytes=64)
         late_view = late_pairs[:].rearrange("v (c q) -> v c q", q=2 * P)
 
         total = bank(3, [P, 1, 4, P])
         turned_sum(total, (0,), 0, V, D, [])
+        look_ahead(1, 2, 0, EARLY)
+        look_ahead(1, 3, 0, EARLY)
+        look_ahead(2, 2, 0, EARLY)
+        look_ahead(2, 3, 0, EARLY)
         nc.scalar.copy(early_view[:, :, 0, 0:P], total[:, 0, 0:2, :])
         nc.scalar.copy(late_view[:, :, 0:P], total[:, 0, 2:4, :])
         total = bank(4, [P, 1, 2, P])
         turned_sum(total, (1,), 0, EARLY, D, [])
+        look_ahead(3, 2, 0, EARLY + P)
+        look_ahead(3, 3, 0, EARLY)
         nc.scalar.copy(early_view[:, :, 0, P : 2 * P], total[:, 0, :, :])
         early_words = early_pairs[:].bitcast(F32)
         backs = [bank(6 + c, [P, 2, P]) for c in range(2)]
@@ -221,6 +232,12 @@ def tile_picked_zwarp_none_po_kernel(
 
         for c in range(2):
             turn_back_early(c, 0)
+        w2_grouped = held.tile([P, N * PACK], BF16, align_bytes=64)
+        nc.scalar.copy(
+            w2_grouped[:].rearrange("p (t m j) -> p m j t", t=PACK, j=PACK),
+            w2_raw[:].rearrange("p j (m t) -> p m j t", t=PACK),
+        )
+        look_ahead(1, 3, EARLY, V)
         total = bank(5, [P, 2, 2, P])
         first_late = bank(2, [P, P])
         for n, t in enumerate((2, 3)):
@@ -234,7 +251,10 @@ def tile_picked_zwarp_none_po_kernel(
             for d in range(D):
                 wide = t == 3 and d < D - 1
                 width = EARLY + P if wide else EARLY
-                term = ring.tile([P, width], F32, name="term")
+                if (t, d) == (3, 2):
+                    term = held.tile([P, width], F32, name="term32", tag="w2_codes", align_bytes=64)
+                else:
+                    term = ring.tile([P, width], F32, name="term")
                 weighted(term[:], t, d, 0, width)
                 for c in range(2):
                     nc.tensor.matmul(
@@ -263,6 +283,10 @@ def tile_picked_zwarp_none_po_kernel(
                 early_grouped[c][:].bitcast(F32).rearrange("p (v u) -> p v u", u=2),
                 backs[c][:].rearrange("p u v -> p v u"),
             )
+        late_looked = held.tile([P, 2 * (V - EARLY)], F32, name="late_looked", tag="early_pairs", align_bytes=64)
+        for d in (1, 2):
+            look_ahead(2, d, EARLY, V, late_looked[:, (d - 1) * (V - EARLY) : d * (V - EARLY)])
+        w2_codes, w2_scales = quantise(w2_grouped, N, "w2", "w2_codes", "w2_scales")
         total = bank(5, [P, 1, 2, P])
         turned_sum(total, (1,), EARLY, V, D, [])
         nc.scalar.copy(late_view[:, :, P : 2 * P], total[:, 0, :, :])
@@ -274,13 +298,13 @@ def tile_picked_zwarp_none_po_kernel(
         slots = [late_terms[:, n * P : (n + 2) * P] for n in (0, 2, 4)] + [late_terms[:, n * P : (n + 1) * P] for n in range(6, 9)]
         y_early = held.tile([P, PACK, EARLY], F32)
         for c in range(2):
-            acc = bank(c, [P, PACK, P])
+            acc = bank(6 + c, [P, PACK, P])
             second_product(acc, *early_planes[c], slice(0, P), range(PACK))
             nc.scalar.copy(y_early[:, :, c * P : (c + 1) * P], acc[:])
         nc.sync.dma_start(out=out_rows[:, :, 0:EARLY], in_=y_early[:])
 
         late_words = late_pairs[:].bitcast(F32)
-        back = bank(3, [P, 2, P])
+        back = bank(1, [P, 2, P])
         for c in range(2):
             nc.tensor.transpose(back[:, c, :], late_words[:, c * P : (c + 1) * P], identity[:])
         late_grouped = [
@@ -294,13 +318,13 @@ def tile_picked_zwarp_none_po_kernel(
             )
 
 
-        partials = [bank(number, [P, 2, P]) for number in (6, 5)]
+        partials = [bank(number, [P, 2, P]) for number in (2, 4)]
         turned = [
             held.tile([P, 2 * P], F32, name="turned2")[:],
             placed.tile([P, P], F32, name="turned_last", align_bytes=64, offset=4608)[:],
         ]
         nc.tensor.transpose(partials[0][:, 1, :], turned3[:], identity[:])
-        parts = ((2, 0, 2, 4), (3, 1, 2, 7))
+        parts = ((2, 0, 2, 3), (3, 1, 2, 0))
         for (t, c0, c1, number), sums in zip(parts, turned):
             total = bank(number, [P, 1, c1 - c0, P])
             turned_sum(total, (t,), EARLY + c0 * P, EARLY + c1 * P, D - 1, slots)
@@ -346,7 +370,7 @@ def tile_picked_zwarp_none_po_kernel(
             v0 = EARLY + c * P
             y_late = held.tile([P, PACK, P], F32, name="y_late%d" % c)
             for h in range(2):
-                acc = bank(((7, 4), (0, 1))[c][h], [P, 2, P])
+                acc = bank(((0, 3), (5, 1))[c][h], [P, 2, P])
                 second_product(acc, late_e_codes[c], late_e_scales[c], slice(0, P), range(2 * h, 2 * h + 2))
                 emptying = nc.vector.tensor_copy if (c, h) == (0, 1) else nc.scalar.copy
                 emptying(y_late[:, 2 * h : 2 * h + 2, :], acc[:])

@@ -114,7 +114,7 @@ def tile_picked_zwarp_none_po_kernel(
                             start=True,
                             stop=True,
                         )
-                if t == 0 and (a, b) in FIRST_PIECES[2:3]:
+                if t == 0 and (a, b) in FIRST_PIECES[1:3]:
                     nc.vector.tensor_scalar_mul(feature[:, a:b], acc[:], -1.0)
                 else:
                     nc.scalar.activation(feature[:, a:b], acc[:], COPY, scale=-1.0)
@@ -208,7 +208,7 @@ def tile_picked_zwarp_none_po_kernel(
 
         early_pairs = held.tile([P, 2 * H], BF16, name="early_pairs", tag="early_pairs", align_bytes=64)
         early_view = early_pairs[:].rearrange("v (c u q) -> v c u q", u=2, q=2 * P)
-        late_pairs = held.tile([P, H], BF16, align_bytes=64)
+        late_pairs = held.tile([P, H], BF16, name="late_pairs", tag="late_pairs", align_bytes=64)
         late_view = late_pairs[:].rearrange("v (c q) -> v c q", q=2 * P)
 
         total = bank(3, [P, 1, 4, P])
@@ -283,12 +283,31 @@ def tile_picked_zwarp_none_po_kernel(
                 early_grouped[c][:].bitcast(F32).rearrange("p (v u) -> p v u", u=2),
                 backs[c][:].rearrange("p u v -> p v u"),
             )
-        late_looked = held.tile([P, 2 * (V - EARLY)], F32, name="late_looked", tag="early_pairs", align_bytes=64)
-        for d in (1, 2):
+        late_looked = held.tile([P, 3 * (V - EARLY)], F32, name="late_looked", tag="early_pairs", align_bytes=64)
+        for d in (1, 2, 3):
             look_ahead(2, d, EARLY, V, late_looked[:, (d - 1) * (V - EARLY) : d * (V - EARLY)])
-        w2_codes, w2_scales = quantise(w2_grouped, N, "w2", "w2_codes", "w2_scales")
         total = bank(5, [P, 1, 2, P])
-        turned_sum(total, (1,), EARLY, V, D, [])
+        for c in range(2):
+            nc.tensor.matmul(
+                total[:, 0, c, :], refs[1][:, EARLY + c * P : EARLY + (c + 1) * P], identity[:],
+                is_transpose=True, start=(c == 0), stop=False,
+            )
+        late_low = [ring.tile([P, V - EARLY], F32, name="term")[:] for d in range(D)]
+
+        def join(d):
+            nc.vector.tensor_tensor(late_low[d], late_low[d], late_low[d + 1], ADD)
+            for c in range(2):
+                nc.tensor.matmul(
+                    total[:, 0, c, :], late_low[d][:, c * P : (c + 1) * P], identity[:],
+                    is_transpose=True, start=False, stop=(d == 2 and c == 1),
+                )
+
+        for d in (0, 1, 3):
+            weighted(late_low[d], 1, d, EARLY, V)
+        join(0)
+        weighted(late_low[2], 1, 2, EARLY, V)
+        w2_codes, w2_scales = quantise(w2_grouped, N, "w2", "w2_codes", "w2_scales")
+        join(2)
         nc.scalar.copy(late_view[:, :, P : 2 * P], total[:, 0, :, :])
 
         early_planes = [
@@ -318,31 +337,35 @@ def tile_picked_zwarp_none_po_kernel(
             )
 
 
-        partials = [bank(number, [P, 2, P]) for number in (2, 4)]
-        turned = [
-            held.tile([P, 2 * P], F32, name="turned2")[:],
-            placed.tile([P, P], F32, name="turned_last", align_bytes=64, offset=4608)[:],
-        ]
-        nc.tensor.transpose(partials[0][:, 1, :], turned3[:], identity[:])
-        parts = ((2, 0, 2, 3), (3, 1, 2, 0))
-        for (t, c0, c1, number), sums in zip(parts, turned):
-            total = bank(number, [P, 1, c1 - c0, P])
-            turned_sum(total, (t,), EARLY + c0 * P, EARLY + c1 * P, D - 1, slots)
-            nc.scalar.copy(sums, total[:].rearrange("v s c p -> v (s c p)"))
-            for c in range(c0, c1):
-                nc.tensor.transpose(partials[c][:, t - 2, :], sums[:, (c - c0) * P : (c - c0 + 1) * P], identity[:])
-
-        first_grouped = placed.tile([P, P * PACK], BF16, name="first_grouped", align_bytes=64, offset=4864)
-        round_for_planes(nc.scalar.copy, first_grouped, y_early[:, :, 0:P])
-        weighted(late_terms[:, 12 * P : 14 * P], 2, D - 1, EARLY, V)
-        for c in range(2):
-            weighted(late_terms[:, (14 + c) * P : (15 + c) * P], 3, D - 1, EARLY + c * P, EARLY + (c + 1) * P)
+        partial = bank(2, [P, 2, P])
+        nc.tensor.transpose(partial[:, 1, :], turned3[:], identity[:])
+        total = bank(3, [P, P])
+        nc.tensor.matmul(total[:], refs[2][:, EARLY : EARLY + P], identity[:], is_transpose=True, start=True, stop=False)
+        for d in range(D - 1):
+            weighted(slots[d], 2, d, EARLY, V)
+            nc.tensor.matmul(total[:], slots[d][:, 0:P], identity[:], is_transpose=True, start=False, stop=(d == D - 2))
+        turned2 = held.tile([P, P], F32)
+        blocks = late_terms[:].rearrange("p (n v) -> p n v", v=P)
+        for d in range(D - 1):
+            weighted(slots[3 + d], 3, d, EARLY + P, V)
+        nc.vector.tensor_copy(turned2[:], total[:])
+        nc.tensor.transpose(partial[:, 0, :], turned2[:], identity[:])
+        early_y_grouped = held.tile([P, EARLY * PACK], BF16, name="early_y_grouped", tag="late_pairs", align_bytes=64)
+        round_for_planes(nc.scalar.copy, early_y_grouped, y_early[:])
+        both = [blocks[:, 2 * d + 1 : 7 + d : 5 - d, :] for d in range(D - 1)]
+        summed = held.tile([P, 2, 2, P], F32)
+        nc.vector.tensor_tensor(summed[:, 0], both[0], ref_high[:, :, EARLY + P : V], ADD)
+        weighted(blocks[:, 12:14, :].rearrange("p n v -> p (n v)"), 2, D - 1, EARLY, V)
+        nc.vector.tensor_tensor(summed[:, 1], both[1], both[2], ADD)
+        weighted(blocks[:, 14, :], 3, D - 1, EARLY, EARLY + P)
+        nc.vector.tensor_tensor(summed[:, 0], summed[:, 0], summed[:, 1], ADD)
+        weighted(blocks[:, 15, :], 3, D - 1, EARLY + P, V)
         last_terms = late_terms[:, 12 * P : 16 * P].rearrange("p (s c v) -> p c v s", s=2, c=2)
-        for c in range(2):
+        for c, rest in enumerate((partial[:], summed[:, 0])):
             nc.vector.tensor_tensor(
                 late_grouped[c][:].rearrange("p (v j) -> p v j", j=PACK)[:, :, 2:4],
                 last_terms[:, c],
-                partials[c][:].rearrange("p s v -> p v s"),
+                rest.rearrange("p s v -> p v s"),
                 ADD,
             )
         late_e_codes = [
@@ -355,13 +378,8 @@ def tile_picked_zwarp_none_po_kernel(
                 out=late_e_codes[c][:].bitcast(FP8X4), scales=late_e_scales[c][:], in_=late_grouped[c][:]
             )
 
-        second_grouped = placed.tile([P, P * PACK], BF16, name="second_grouped", align_bytes=64, offset=2560)
-        round_for_planes(nc.vector.tensor_copy, second_grouped, y_early[:, :, P:EARLY])
         y_codes = placed.tile([P, EARLY], I32, name="y_early_codes", align_bytes=64, offset=1536)
-        for c, grouped in enumerate((first_grouped, second_grouped)):
-            nc.vector.quantize_mx(
-                out=y_codes[:, c * P : (c + 1) * P].bitcast(FP8X4), scales=y_scales[:, c * P : (c + 1) * P], in_=grouped[:]
-            )
+        nc.vector.quantize_mx(out=y_codes[:].bitcast(FP8X4), scales=y_scales[:, 0:EARLY], in_=early_y_grouped[:])
         nc.sync.dma_start(out=out_words[:, 0:EARLY], in_=y_codes[:])
 
         late_codes = held.tile([P, V - EARLY], I32, align_bytes=64)

@@ -294,20 +294,17 @@ def tile_picked_zwarp_none_po_kernel(
             )
         late_low = [ring.tile([P, V - EARLY], F32, name="term")[:] for d in range(D)]
 
-        def join(d):
-            nc.vector.tensor_tensor(late_low[d], late_low[d], late_low[d + 1], ADD)
+        for d in (3, 2, 0):
+            weighted(late_low[d], 1, d, EARLY, V)
+        nc.vector.tensor_tensor(late_low[2], late_low[2], late_low[3], ADD)
+        weighted(late_low[1], 1, 1, EARLY, V)
+        for d in (2, 0, 1):
             for c in range(2):
                 nc.tensor.matmul(
                     total[:, 0, c, :], late_low[d][:, c * P : (c + 1) * P], identity[:],
-                    is_transpose=True, start=False, stop=(d == 2 and c == 1),
+                    is_transpose=True, start=False, stop=(d == 1 and c == 1),
                 )
-
-        for d in (0, 1, 3):
-            weighted(late_low[d], 1, d, EARLY, V)
-        join(0)
-        weighted(late_low[2], 1, 2, EARLY, V)
         w2_codes, w2_scales = quantise(w2_grouped, N, "w2", "w2_codes", "w2_scales")
-        join(2)
         nc.scalar.copy(late_view[:, :, P : 2 * P], total[:, 0, :, :])
 
         early_planes = [

@@ -222,7 +222,7 @@ def tile_picked_zwarp_none_po_kernel(
         total = bank(4, [P, 1, 2, P])
         turned_sum(total, (1,), 0, EARLY, D, [])
         look_ahead(3, 2, 0, EARLY + P)
-        look_ahead(3, 3, 0, EARLY)
+        look_ahead(3, 3, 0, EARLY, held.tile([P, EARLY], F32, name="looked3_3", tag="looked3_3", align_bytes=64)[:])
         nc.scalar.copy(early_view[:, :, 0, P : 2 * P], total[:, 0, :, :])
         early_words = early_pairs[:].bitcast(F32)
         backs = [bank(6 + c, [P, 2, P]) for c in range(2)]
@@ -274,13 +274,11 @@ def tile_picked_zwarp_none_po_kernel(
                 total[:, :, c, :].rearrange("v s p -> v p s"),
             )
             turn_back_early(c, 1)
-        early_grouped = [
-            held.tile([P, P * PACK], BF16, name="early_grouped%d" % c, tag="early_shared%d" % c, align_bytes=64)
-            for c in range(2)
-        ]
+        late_terms = held.tile([P, 16 * P], F32, name="late_terms", tag="looked3_3", align_bytes=64)
+        early_grouped = [late_terms[:, n * P : (n + 2) * P] for n in (0, 14)]
         for c in range(2):
             nc.scalar.copy(
-                early_grouped[c][:].bitcast(F32).rearrange("p (v u) -> p v u", u=2),
+                early_grouped[c].rearrange("p (v u) -> p v u", u=2),
                 backs[c][:].rearrange("p u v -> p v u"),
             )
         late_looked = held.tile([P, 3 * (V - EARLY)], F32, name="late_looked", tag="early_pairs", align_bytes=64)
@@ -307,11 +305,12 @@ def tile_picked_zwarp_none_po_kernel(
         w2_codes, w2_scales = quantise(w2_grouped, N, "w2", "w2_codes", "w2_scales")
         nc.scalar.copy(late_view[:, :, P : 2 * P], total[:, 0, :, :])
 
-        early_planes = [
-            quantise(early_grouped[c], P, "e_early%d" % c, "e_early_codes%d" % c, "e_early_scales%d" % c) for c in range(2)
-        ]
-        late_terms = held.tile([P, 16 * P], F32, name="late_terms", tag="early_shared0", align_bytes=64)
         slots = [late_terms[:, n * P : (n + 2) * P] for n in (0, 2, 4)] + [late_terms[:, n * P : (n + 1) * P] for n in range(6, 9)]
+        for d in range(D - 1):
+            weighted(slots[3 + d], 3, d, EARLY + P, V)
+        early_planes = [
+            quantise(early_grouped[c].bitcast(BF16), P, "e_early%d" % c, "e_early_codes%d" % c, "e_early_scales%d" % c) for c in range(2)
+        ]
         y_early = held.tile([P, PACK, EARLY], F32)
         for c in range(2):
             acc = bank(6 + c, [P, PACK, P])
@@ -319,6 +318,13 @@ def tile_picked_zwarp_none_po_kernel(
             nc.scalar.copy(y_early[:, :, c * P : (c + 1) * P], acc[:])
         nc.sync.dma_start(out=out_rows[:, :, 0:EARLY], in_=y_early[:])
 
+        partial = bank(2, [P, 2, P])
+        nc.tensor.transpose(partial[:, 1, :], turned3[:], identity[:])
+        total = bank(3, [P, P])
+        nc.tensor.matmul(total[:], refs[2][:, EARLY : EARLY + P], identity[:], is_transpose=True, start=True, stop=False)
+        for d in range(D - 1):
+            weighted(slots[d], 2, d, EARLY, V)
+            nc.tensor.matmul(total[:], slots[d][:, 0:P], identity[:], is_transpose=True, start=False, stop=(d == D - 2))
         late_words = late_pairs[:].bitcast(F32)
         back = bank(1, [P, 2, P])
         for c in range(2):
@@ -332,21 +338,8 @@ def tile_picked_zwarp_none_po_kernel(
                 late_grouped[c][:].bitcast(F32).rearrange("p (v u) -> p v u", u=2),
                 back[:, c, :].unsqueeze(2).to_broadcast([P, P, 2]),
             )
-
-
-        partial = bank(2, [P, 2, P])
-        nc.tensor.transpose(partial[:, 1, :], turned3[:], identity[:])
-        total = bank(3, [P, P])
-        nc.tensor.matmul(total[:], refs[2][:, EARLY : EARLY + P], identity[:], is_transpose=True, start=True, stop=False)
-        for d in range(D - 1):
-            weighted(slots[d], 2, d, EARLY, V)
-            nc.tensor.matmul(total[:], slots[d][:, 0:P], identity[:], is_transpose=True, start=False, stop=(d == D - 2))
         turned2 = held.tile([P, P], F32)
         blocks = late_terms[:].rearrange("p (n v) -> p n v", v=P)
-        for d in range(D - 1):
-            weighted(slots[3 + d], 3, d, EARLY + P, V)
-        nc.vector.tensor_copy(turned2[:], total[:])
-        nc.tensor.transpose(partial[:, 0, :], turned2[:], identity[:])
         early_y_grouped = held.tile([P, EARLY * PACK], BF16, name="early_y_grouped", tag="late_pairs", align_bytes=64)
         round_for_planes(nc.scalar.copy, early_y_grouped, y_early[:])
         both = [blocks[:, 2 * d + 1 : 7 + d : 5 - d, :] for d in range(D - 1)]
@@ -354,6 +347,8 @@ def tile_picked_zwarp_none_po_kernel(
         nc.vector.tensor_tensor(summed[:, 0], both[0], ref_high[:, :, EARLY + P : V], ADD)
         weighted(blocks[:, 12:14, :].rearrange("p n v -> p (n v)"), 2, D - 1, EARLY, V)
         nc.vector.tensor_tensor(summed[:, 1], both[1], both[2], ADD)
+        nc.vector.tensor_copy(turned2[:], total[:])
+        nc.tensor.transpose(partial[:, 0, :], turned2[:], identity[:])
         weighted(blocks[:, 14, :], 3, D - 1, EARLY, EARLY + P)
         nc.vector.tensor_tensor(summed[:, 0], summed[:, 0], summed[:, 1], ADD)
         weighted(blocks[:, 15, :], 3, D - 1, EARLY + P, V)

from contextlib import ExitStack

import concourse.mybir as mybir
from concourse.masks import make_identity

K, T, S, D, V, H, N = 512, 2048, 1024, 4, 512, 512, 512
FLOPS = 2 * K * H * S + 2 * H * N * V

F32 = mybir.dt.float32
BF16 = mybir.dt.bfloat16
I32 = mybir.dt.int32
U32 = mybir.dt.uint32
U16 = mybir.dt.uint16
U8 = mybir.dt.uint8
FP8X4 = mybir.dt.float8_e4m3fn_x4
COPY = mybir.ActivationFunctionType.Copy
MULT = mybir.AluOpType.mult
ADD = mybir.AluOpType.add

P = 128
PACK = 4
STRIPE = 16
EARLY = 256
WORD_PIECES = ((0, 512), (512, 768), (768, 1024))
FIRST_PIECES = ((0, 512), (512, 768), (768, 896), (896, 1024))
HALVES = ((0, 512), (512, 1024))


def tile_picked_zwarp_none_po_kernel(
    tc, x_words, x_scales, w1, w2, gate, ref, offs, pos1, pos2, pos3, pos4, out_0, out_1, out_2
):
    nc = tc.nc
    with ExitStack() as ctx:
        held = ctx.enter_context(tc.tile_pool(name="held", bufs=1))
        ring = ctx.enter_context(tc.tile_pool(name="ring", bufs=8))
        placed = ctx.enter_context(tc.tile_pool(name="placed", bufs=1))
        psum = ctx.enter_context(tc.psum_pool(name="psum", bufs=1))

        def bank(number, shape):
            return psum.tile(shape, F32, name="bank%d" % number, tag="bank%d" % number)

        scale_table = held.tile([P, T], U8, align_bytes=64)
        nc.gpsimd.memset(scale_table[:].bitcast(I32), 0)
        picks = held.tile([P, S // STRIPE], U16)
        nc.sync.dma_start(picks[:], offs)
        corners = [held.tile([P, V // STRIPE], U16, name="corner%d" % d) for d in range(D)]
        nc.sync.dma_start(corners[0][:], pos1)
        for r in range(4):
            nc.sync.dma_start(
                out=scale_table[r:P:32, :].bitcast(I32),
                in_=x_scales[0, r:16:4, :].bitcast(I32),
            )
        word_table = held.tile([P, T], I32, align_bytes=64)
        nc.sync.dma_start(out=word_table[:], in_=x_words[0].rearrange("p c r -> p (c r)").bitcast(I32))
        w1_rows = w1.rearrange("(p j) h -> p j h", j=PACK)
        w1_halves = [held.tile([P, PACK, H // 2], F32, name="w1_half%d" % h) for h in range(2)]
        nc.sync.dma_start(out=w1_halves[0][:], in_=w1_rows[:, :, 0 : H // 2])
        gates = [held.tile([P, V], F32, name="gate%d" % d, align_bytes=64) for d in range(D)]
        ref_low = [held.tile([P, V], F32, name="ref_low%d" % h) for h in range(2)]
        ref_low_rows = ref.rearrange("(h m r) v -> h m r v", h=2, r=PACK)
        ref_high = held.tile([P, 2, V], F32)
        nc.sync.dma_start(out=w1_halves[1][:], in_=w1_rows[:, :, H // 2 : H])
        nc.sync.dma_start(out=gates[0][:], in_=gate[0])
        nc.sync.dma_start(corners[1][:], pos2)
        nc.sync.dma_start(out=gates[1][:], in_=gate[1])
        nc.sync.dma_start(out=ref_low[0][:], in_=ref_low_rows[0, :, 0:2, :])
        for d, pos in ((2, pos3), (3, pos4)):
            nc.sync.dma_start(corners[d][:], pos)
            nc.sync.dma_start(out=gates[d][:], in_=gate[d])
        nc.sync.dma_start(out=ref_low[1][:], in_=ref_low_rows[1, :, 0:2, :])
        nc.sync.dma_start(out=ref_high[:], in_=ref.rearrange("(p r) v -> p r v", r=PACK)[:, 2:4, :])
        w2_raw = held.tile([P, PACK, N], F32)
        nc.sync.dma_start(out=w2_raw[:], in_=w2.rearrange("(p j) n -> p j n", j=PACK))
        refs = [ref_low[0][:], ref_low[1][:], ref_high[:, 0, :], ref_high[:, 1, :]]

        identity = held.tile([P, P], F32)
        make_identity(nc, identity[:])

        x_bytes = held.tile([P, S], U8, align_bytes=64)
        nc.vector.tensor_copy(x_bytes[:], scale_table[:].indirect(picks[:]))
        x_codes = {}

        def gather_words(a, b, tile):
            x_codes[a] = tile
            nc.vector.tensor_copy(
                x_codes[a][:], word_table[:].bitcast(U32).indirect(picks[:, a // STRIPE : b // STRIPE])
            )

        for a, b in WORD_PIECES[:-1]:
            gather_words(a, b, held.tile([P, b - a], U32, name="x_codes%d" % a, align_bytes=64))

        features = []
        first_banks = [0, 1, 4, 3, 2, 5, 6, 7, 0, 1]

        def quantise(grouped, width, name, codes_tag, scales_tag):
            codes = held.tile([P, width], U32, name=name + "_codes", tag=codes_tag, align_bytes=64)
            scales = held.tile([P, width], U8, name=name + "_scales", tag=scales_tag, align_bytes=64)
            nc.vector.quantize_mx(out=codes[:].bitcast(FP8X4), scales=scales[:], in_=grouped[:])
            return codes, scales

        def first_product(t, codes, scales, cols):
            feature = held.tile([P, S], F32, name="feature%d" % t)
            for a, b in FIRST_PIECES if t == 0 else HALVES:
                acc = bank(first_banks.pop(0), [P, b - a])
                for pa, pb in WORD_PIECES:
                    lo, hi = max(a, pa), min(b, pb)
                    if lo < hi:
                        nc.tensor.matmul_mx(
                            out=acc[:, lo - a : hi - a],
                            lhsT=codes[:, cols].bitcast(FP8X4),
                            lhsT_scale=scales[:, cols],
                            rhs=x_codes[pa][:, lo - pa : hi - pa].bitcast(FP8X4),
                            rhs_scale=x_bytes[:, lo:hi],
                            start=True,
                            stop=True,
                        )
                if t == 0 and (a, b) in FIRST_PIECES[1:3]:
                    nc.vector.tensor_scalar_mul(feature[:, a:b], acc[:], -1.0)
                else:
                    nc.scalar.activation(feature[:, a:b], acc[:], COPY, scale=-1.0)
            features.append(feature)

        low_grouped = [
            placed.tile([P, P * PACK], BF16, name="w1_low%d" % h, align_bytes=64, offset=8704 - 512 * h) for h in range(2)
        ]
        high_grouped = held.tile([P, 2 * P * PACK], BF16, align_bytes=64)

        def round_low(copy, h):
            copy(
                low_grouped[h][:].rearrange("p (m e j) -> p m j e", e=2, j=PACK),
                w1_halves[h][:].rearrange("p j (m r) -> p m j r", r=PACK)[:, :, :, 0:2],
            )

        def round_high(h):
            nc.scalar.copy(
                high_grouped[:].rearrange("p (s h m j) -> p h m j s", s=2, h=2, j=PACK)[:, h],
                w1_halves[h][:].rearrange("p j (m r) -> p m j r", r=PACK)[:, :, :, 2:4],
            )

        round_low(nc.scalar.copy, 0)
        round_high(0)
        round_high(1)
        codes, scales = quantise(low_grouped[0], P, "w1_low0", "w1_codes0", "w1_scales0")
        gather_words(*WORD_PIECES[-1], placed.tile([P, 256], U32, name="x_codes_last", align_bytes=64, offset=9216))
        first_product(0, codes, scales, slice(0, P))
        round_low(nc.vector.tensor_copy, 1)
        codes, scales = quantise(low_grouped[1], P, "w1_low1", "w1_codes1", "w1_scales1")
        first_product(1, codes, scales, slice(0, P))
        codes, scales = quantise(high_grouped, 2 * P, "w1_high", "w1_codes2", "w1_scales2")
        for s in range(2):
            first_product(2 + s, codes, scales, slice(s * P, (s + 1) * P))

        out_rows = out_0.rearrange("(p t) v -> p t v", t=PACK)
        out_words = out_1[0].rearrange("p c r -> p (c r)").bitcast(I32)
        y_scales = held.tile([P, V], U8, align_bytes=64)

        looked = {}

        def fetched(t, d, v0, v1):
            return features[t][:].indirect(corners[d][:, v0 // STRIPE : v1 // STRIPE])

        def look_ahead(t, d, v0, v1, into=None):
            if into is None:
                into = held.tile([P, v1 - v0], F32, name="looked%d_%d_%d" % (t, d, v0))[:]
            looked[t, d, v0] = into
            nc.scalar.activation(into, fetched(t, d, v0, v1), COPY)

        def weighted(term, t, d, v0, v1):
            values = looked[t, d, v0] if (t, d, v0) in looked else fetched(t, d, v0, v1)
            nc.vector.tensor_tensor(term, values, gates[d][:, v0:v1], MULT)

        def turned_sum(total, tiles, v0, v1, corner_count, slots):
            chunks = (v1 - v0) // P
            for n, t in enumerate(tiles):
                for c in range(chunks):
                    nc.tensor.matmul(
                        total[:, n, c, :], refs[t][:, v0 + c * P : v0 + (c + 1) * P], identity[:],
                        is_transpose=True, start=(n == 0 and c == 0), stop=False,
                    )
            for n, t in enumerate(tiles):
                for d in range(corner_count):
                    term = slots.pop(0) if slots else ring.tile([P, v1 - v0], F32, name="term")[:]
                    weighted(term, t, d, v0, v1)
                    for c in range(chunks):
                        nc.tensor.matmul(
                            total[:, n, c, :], term[:, c * P : (c + 1) * P], identity[:],
                            is_transpose=True, start=False,
                            stop=(n == len(tiles) - 1 and d == corner_count - 1 and c == chunks - 1),
                        )

        def second_product(acc, e_codes, e_scales, cols, out_tiles):
            for n, t in enumerate(out_tiles):
                nc.tensor.matmul_mx(
                    out=acc[:, n, :],
                    lhsT=w2_codes[:, t * P : (t + 1) * P].bitcast(FP8X4),
                    lhsT_scale=w2_scales[:, t * P : (t + 1) * P],
                    rhs=e_codes[:, cols].bitcast(FP8X4),
                    rhs_scale=e_scales[:, cols],
                    start=True,
                    stop=True,
                )

        def round_for_planes(copy, grouped, y):
            copy(
                grouped[:].rearrange("p (c i t) -> p c t i", i=4, t=PACK),
                y.rearrange("p t (c i) -> p c t i", i=4),
            )

        early_pairs = held.tile([P, 2 * H], BF16, name="early_pairs", tag="early_pairs", align_bytes=64)
        early_view = early_pairs[:].rearrange("v (c u q) -> v c u q", u=2, q=2 * P)
        late_pairs = held.tile([P, H], BF16, name="late_pairs", tag="late_pairs", align_bytes=64)
        late_view = late_pairs[:].rearrange("v (c q) -> v c q", q=2 * P)

        total = bank(3, [P, 1, 4, P])
        turned_sum(total, (0,), 0, V, D, [])
        look_ahead(1, 2, 0, EARLY)
        look_ahead(1, 3, 0, EARLY)
        look_ahead(2, 2, 0, EARLY)
        look_ahead(2, 3, 0, EARLY)
        nc.scalar.copy(early_view[:, :, 0, 0:P], total[:, 0, 0:2, :])
        nc.scalar.copy(late_view[:, :, 0:P], total[:, 0, 2:4, :])
        total = bank(4, [P, 1, 2, P])
        turned_sum(total, (1,), 0, EARLY, D, [])
        look_ahead(3, 2, 0, EARLY + P)
        look_ahead(3, 3, 0, EARLY, held.tile([P, EARLY], F32, name="looked3_3", tag="looked3_3", align_bytes=64)[:])
        nc.scalar.copy(early_view[:, :, 0, P : 2 * P], total[:, 0, :, :])
        early_words = early_pairs[:].bitcast(F32)
        backs = [bank(6 + c, [P, 2, P]) for c in range(2)]

        def turn_back_early(c, u):
            nc.tensor.transpose(backs[c][:, u, :], early_words[:, (2 * c + u) * P : (2 * c + u + 1) * P], identity[:])

        for c in range(2):
            turn_back_early(c, 0)
        w2_grouped = held.tile([P, N * PACK], BF16, align_bytes=64)
        nc.scalar.copy(
            w2_grouped[:].rearrange("p (t m j) -> p m j t", t=PACK, j=PACK),
            w2_raw[:].rearrange("p j (m t) -> p m j t", t=PACK),
        )
        look_ahead(1, 3, EARLY, V)
        total = bank(5, [P, 2, 2, P])
        first_late = bank(2, [P, P])
        for n, t in enumerate((2, 3)):
            for c in range(2):
                nc.tensor.matmul(
                    total[:, n, c, :], refs[t][:, c * P : (c + 1) * P], identity[:],
                    is_transpose=True, start=(n == 0 and c == 0), stop=False,
                )
        nc.tensor.matmul(first_late[:], refs[3][:, EARLY : EARLY + P], identity[:], is_transpose=True, start=True, stop=False)
        for n, t in enumerate((2, 3)):
            for d in range(D):
                wide = t == 3 and d < D - 1
                width = EARLY + P if wide else EARLY
                if (t, d) == (3, 2):
                    term = held.tile([P, width], F32, name="term32", tag="w2_codes", align_bytes=64)
                else:
                    term = ring.tile([P, width], F32, name="term")
                weighted(term[:], t, d, 0, width)
                for c in range(2):
                    nc.tensor.matmul(
                        total[:, n, c, :], term[:, c * P : (c + 1) * P], identity[:],
                        is_transpose=True, start=False, stop=(t == 3 and d == D - 1 and c == 1),
                    )
                if wide:
                    nc.tensor.matmul(
                        first_late[:], term[:, EARLY : EARLY + P], identity[:],
                        is_transpose=True, start=False, stop=(d == D - 2),
                    )
        turned3 = held.tile([P, P], F32)
        nc.scalar.copy(turned3[:], first_late[:])
        for c in range(2):
            nc.scalar.copy(
                early_view[:, c, 1, :].rearrange("v (p s) -> v p s", s=2),
                total[:, :, c, :].rearrange("v s p -> v p s"),
            )
            turn_back_early(c, 1)
        late_terms = held.tile([P, 16 * P], F32, name="late_terms", tag="looked3_3", align_bytes=64)
        early_grouped = [late_terms[:, n * P : (n + 2) * P] for n in (0, 14)]
        for c in range(2):
            nc.scalar.copy(
                early_grouped[c].rearrange("p (v u) -> p v u", u=2),
                backs[c][:].rearrange("p u v -> p v u"),
            )
        late_looked = held.tile([P, 3 * (V - EARLY)], F32, name="late_looked", tag="early_pairs", align_bytes=64)
        for d in (1, 2, 3):
            look_ahead(2, d, EARLY, V, late_looked[:, (d - 1) * (V - EARLY) : d * (V - EARLY)])
        total = bank(5, [P, 1, 2, P])
        for c in range(2):
            nc.tensor.matmul(
                total[:, 0, c, :], refs[1][:, EARLY + c * P : EARLY + (c + 1) * P], identity[:],
                is_transpose=True, start=(c == 0), stop=False,
            )
        late_low = [ring.tile([P, V - EARLY], F32, name="term")[:] for d in range(D)]

        for d in (3, 2, 0):
            weighted(late_low[d], 1, d, EARLY, V)
        nc.vector.tensor_tensor(late_low[2], late_low[2], late_low[3], ADD)
        weighted(late_low[1], 1, 1, EARLY, V)
        for d in (2, 0, 1):
            for c in range(2):
                nc.tensor.matmul(
                    total[:, 0, c, :], late_low[d][:, c * P : (c + 1) * P], identity[:],
                    is_transpose=True, start=False, stop=(d == 1 and c == 1),
                )
        w2_codes, w2_scales = quantise(w2_grouped, N, "w2", "w2_codes", "w2_scales")
        nc.scalar.copy(late_view[:, :, P : 2 * P], total[:, 0, :, :])

        slots = [late_terms[:, n * P : (n + 2) * P] for n in (0, 2, 4)] + [late_terms[:, n * P : (n + 1) * P] for n in range(6, 9)]
        for d in range(D - 1):
            weighted(slots[3 + d], 3, d, EARLY + P, V)
        early_planes = [
            quantise(early_grouped[c].bitcast(BF16), P, "e_early%d" % c, "e_early_codes%d" % c, "e_early_scales%d" % c) for c in range(2)
        ]
        y_early = held.tile([P, PACK, EARLY], F32)
        for c in range(2):
            acc = bank(6 + c, [P, PACK, P])
            second_product(acc, *early_planes[c], slice(0, P), range(PACK))
            nc.scalar.copy(y_early[:, :, c * P : (c + 1) * P], acc[:])
        nc.sync.dma_start(out=out_rows[:, :, 0:EARLY], in_=y_early[:])

        partial = bank(2, [P, 2, P])
        nc.tensor.transpose(partial[:, 1, :], turned3[:], identity[:])
        total = bank(3, [P, P])
        nc.tensor.matmul(total[:], refs[2][:, EARLY : EARLY + P], identity[:], is_transpose=True, start=True, stop=False)
        for d in range(D - 1):
            weighted(slots[d], 2, d, EARLY, V)
            nc.tensor.matmul(total[:], slots[d][:, 0:P], identity[:], is_transpose=True, start=False, stop=(d == D - 2))
        late_words = late_pairs[:].bitcast(F32)
        back = bank(1, [P, 2, P])
        for c in range(2):
            nc.tensor.transpose(back[:, c, :], late_words[:, c * P : (c + 1) * P], identity[:])
        late_grouped = [
            held.tile([P, P * PACK], BF16, name="late_grouped0", align_bytes=64),
            placed.tile([P, P * PACK], BF16, name="late_grouped1", align_bytes=64, offset=2048),
        ]
        for c in range(2):
            nc.scalar.copy(
                late_grouped[c][:].bitcast(F32).rearrange("p (v u) -> p v u", u=2),
                back[:, c, :].unsqueeze(2).to_broadcast([P, P, 2]),
            )
        turned2 = held.tile([P, P], F32)
        blocks = late_terms[:].rearrange("p (n v) -> p n v", v=P)
        early_y_grouped = held.tile([P, EARLY * PACK], BF16, name="early_y_grouped", tag="late_pairs", align_bytes=64)
        round_for_planes(nc.scalar.copy, early_y_grouped, y_early[:])
        both = [blocks[:, 2 * d + 1 : 7 + d : 5 - d, :] for d in range(D - 1)]
        summed = held.tile([P, 2, 2, P], F32)
        nc.vector.tensor_tensor(summed[:, 0], both[0], ref_high[:, :, EARLY + P : V], ADD)
        weighted(blocks[:, 12:14, :].rearrange("p n v -> p (n v)"), 2, D - 1, EARLY, V)
        nc.vector.tensor_tensor(summed[:, 1], both[1], both[2], ADD)
        nc.vector.tensor_copy(turned2[:], total[:])
        nc.tensor.transpose(partial[:, 0, :], turned2[:], identity[:])
        weighted(blocks[:, 14, :], 3, D - 1, EARLY, EARLY + P)
        nc.vector.tensor_tensor(summed[:, 0], summed[:, 0], summed[:, 1], ADD)
        weighted(blocks[:, 15, :], 3, D - 1, EARLY + P, V)
        last_terms = late_terms[:, 12 * P : 16 * P].rearrange("p (s c v) -> p c v s", s=2, c=2)
        for c, rest in enumerate((partial[:], summed[:, 0])):
            nc.vector.tensor_tensor(
                late_grouped[c][:].rearrange("p (v j) -> p v j", j=PACK)[:, :, 2:4],
                last_terms[:, c],
                rest.rearrange("p s v -> p v s"),
                ADD,
            )
        late_e_codes = [
            placed.tile([P, P], U32, name="late_e_codes0", align_bytes=64, offset=4352),
            held.tile([P, P], U32, name="late_e_codes1", align_bytes=64),
        ]
        late_e_scales = [held.tile([P, P], U8, name="late_e_scales%d" % c, align_bytes=64) for c in range(2)]
        for c in range(2):
            nc.vector.quantize_mx(
                out=late_e_codes[c][:].bitcast(FP8X4), scales=late_e_scales[c][:], in_=late_grouped[c][:]
            )

        y_codes = placed.tile([P, EARLY], I32, name="y_early_codes", align_bytes=64, offset=1536)
        nc.vector.quantize_mx(out=y_codes[:].bitcast(FP8X4), scales=y_scales[:, 0:EARLY], in_=early_y_grouped[:])
        nc.sync.dma_start(out=out_words[:, 0:EARLY], in_=y_codes[:])

        late_codes = held.tile([P, V - EARLY], I32, align_bytes=64)
        y_late_grouped = [held.tile([P, P * PACK], BF16, name="y_late_grouped%d" % c, align_bytes=64) for c in range(2)]
        for c in range(2):
            v0 = EARLY + c * P
            y_late = held.tile([P, PACK, P], F32, name="y_late%d" % c)
            for h in range(2):
                acc = bank(((0, 3), (5, 1))[c][h], [P, 2, P])
                second_product(acc, late_e_codes[c], late_e_scales[c], slice(0, P), range(2 * h, 2 * h + 2))
                emptying = nc.vector.tensor_copy if (c, h) == (0, 1) else nc.scalar.copy
                emptying(y_late[:, 2 * h : 2 * h + 2, :], acc[:])
            (nc.sync if c == 0 else nc.scalar).dma_start(out=out_rows[:, :, v0 : v0 + P], in_=y_late[:])
            round_for_planes(nc.vector.tensor_copy, y_late_grouped[c], y_late[:])
        for c in range(2):
            v0 = EARLY + c * P
            nc.vector.quantize_mx(
                out=late_codes[:, c * P : (c + 1) * P].bitcast(FP8X4), scales=y_scales[:, v0 : v0 + P],
                in_=y_late_grouped[c][:],
            )
        nc.sync.dma_start(out=out_words[:, EARLY:V], in_=late_codes[:])
        for r in range(4):
            (nc.sync if r < 2 else nc.scalar).dma_start(
                out=out_2[0, r:16:4, :].bitcast(I32),
                in_=y_scales[r:P:32, :].bitcast(I32),
            )
